import numpy as np, ml_dtypes
CORES = [24,25,26,27,28,29,30,31]
N = 8
import mx_ref
BF = ml_dtypes.bfloat16
def gentries(a):
    return np.ascontiguousarray(a.reshape(8, 16, -1).transpose(0, 2, 1)).reshape(8, -1)
def gtable(e):
    e = np.asarray(e); return np.ascontiguousarray(e.reshape(8, -1, 16).transpose(0, 2, 1)).reshape(128, -1).astype(np.int32)
def gcols(t, e):
    v = np.concatenate([t.reshape(8, 16, -1, 4), np.zeros((8, 16, 1, 4), BF)], axis=2)
    return np.ascontiguousarray(np.stack([v[g][:, e[g]] for g in range(8)])).reshape(128, -1)
def gpick(z, e):
    return np.concatenate([z[16 * g:16 * g + 16][:, e[g]] for g in range(8)])
def tile(rs):
    return np.stack(rs, axis=2).reshape(128, -1).astype(BF)
def pick(q, e):
    c = np.concatenate([q[0].reshape(128, -1, 4), np.zeros((128, 1, 4), np.uint8)], axis=1); s = np.concatenate([q[1], np.ones((16, 1), np.uint8)], axis=1)
    return (np.ascontiguousarray(c[:, e].reshape(128, -1)), np.ascontiguousarray(s[:, e]))
def join(*qs):
    return (np.concatenate([q[0] for q in qs], axis=1), np.concatenate([q[1] for q in qs], axis=1))
def put(q, e, v):
    c, s = q[0].reshape(128, -1, 4).copy(), q[1].copy(); c[:, e] = v[0].reshape(128, -1, 4); s[:, e] = v[1]
    return (c.reshape(128, -1), s)
def pk(c, s):
    return (np.ascontiguousarray(c), mx_ref.live(s))
def emit(q):
    return q[0], q[1]
def packed(v, rng):
    q = [mx_ref.quantize(np.ascontiguousarray(v[r])) for r in range(N)]
    return np.stack([a for a, b in q]), np.stack([mx_ref.plane(b, rng) for a, b in q])
def values_of_codes():
    e, c = np.zeros((128, 128, 4), np.float32), np.zeros((128, 2, 4), np.uint8)
    e[np.arange(128), np.arange(128), 0] = 1
    c[:127, :, 0] = np.arange(256).reshape(2, 128).T[:127]
    return mx_ref.matmul(mx_ref.quantize(e.reshape(128, 512).astype(BF)), (c.reshape(128, 8), np.full((16, 2), 127, np.uint8))).T.reshape(-1).astype(np.float64)
CODE_VALUE, SCALE_VALUE = values_of_codes(), 2.0 ** (np.arange(256) - 127.0)
def decode(q):
    return (CODE_VALUE[q[0]].reshape(16, 8, -1, 4) * SCALE_VALUE[q[1]][:, None, :, None] + 0.0).reshape(128, -1).astype(np.float32)
def f(rng, *shape):
    return mx_ref.flush((rng.standard_normal(shape, dtype=np.float32) * np.exp2(rng.integers(-2, 3, shape[:-1] + (1,)))).astype(BF))
def wide(rng, *shape, cols=0):
    v = rng.standard_normal(shape, dtype=np.float32) * np.exp2(rng.integers(-12, 13, shape)).astype(np.float32)
    if cols: v *= np.repeat(np.exp2(rng.integers(-cols, cols + 1, shape[:-2] + (1, shape[-1] // 4))) * (rng.random(shape[:-2] + (1, shape[-1] // 4)) > 0.0625), 4, axis=-1).astype(np.float32)
    return mx_ref.flush(v.astype(BF))
C = 320
STEP = [1, 2, 4]
def numbers_of(rng):
    return {"x": np.array(f(rng, N, 128, 4 * C)), "u": np.array(f(rng, N, 128, 512)), "v": np.array(f(rng, N, 128, 512))}
def orders(rng):
    return rng.permuted(np.tile(np.arange(C), (N, 8, 1)), axis=2), rng.permuted(np.tile(np.arange(8)[:, None], (N, 1, C)), axis=1)
def stored(p, o):
    return {"pg": np.stack([gtable(p[r]) for r in range(N)]), "og": np.stack([gtable(o[r]) for r in range(N)])}
def layers(rng, still=[]):
    w = np.array(f(rng, N, 128, 2048)).reshape(N, 8, 16, 4, 8, 16, 4)
    for i in still:
        w[:, :, i] = 0
        w[:, :, :, :, :, i] = 0
    return w
def weights(rng, w):
    c, s = packed(np.ascontiguousarray(w).reshape(N, 128, 2048), rng)
    return {"wc": c, "ws": s}
def setup_inputs(rng):
    return {**numbers_of(rng), **stored(*orders(rng)), **weights(rng, layers(rng))}
def setup_inputs_ties(rng):
    d = numbers_of(rng)
    n = rng.permutation(N)
    k = rng.integers(0, 4, (N, 8, C))
    k[n[1]] -= 4
    k[n[2]] = np.arange(8)[:, None]
    x = d["x"].reshape(N, 8, 16, C, 4)
    x[:, :, 0] = 0
    x[:, :, 0, :, 0] = k.astype(np.float32).astype(BF)
    u = d["u"].reshape(N, 128, 128, 4)
    u[:, :, ::16] = 0
    for r in range(N):
        for h in range(0, 128, 16): u[r, h, h, 0] = 0.0 if r == n[0] else 1.0
    p, o = orders(rng)
    o[n[2]] = 7 - np.arange(8)[:, None]
    return {"x": x.reshape(N, 128, 4 * C), "u": u.reshape(N, 128, 512), "v": d["v"], **stored(p, o), **weights(rng, layers(rng, [0]))}
def setup_inputs_near(rng):
    d = numbers_of(rng)
    x = d["x"].astype(np.float32).reshape(N, 8, 16, C, 4)
    x[:, :, 0] = 0
    x[:, :, 8:] = 0
    u = d["u"].reshape(N, 128, 128, 4)
    u[:, :, ::16] = 0
    w = layers(rng, [0, 8, 9, 10, 11, 12, 13, 14, 15])
    kind, size, least = np.zeros(N, np.int64), np.ones(N), 2.0 ** -30
    turn = rng.integers(2)
    for i, r in enumerate(rng.permutation([r for r in range(N) if r < r ^ STEP[0]])):
        both = [r, r ^ STEP[0]]
        kind[both] = 2 if i == 0 else rng.permutation(2)
        size[both] = least if (i + turn) % 2 else 1.0
    for r in range(N):
        s = rng.integers(0, 16, (8, C))
        digits = ((s[:, :, None] >> np.arange(4)) & 1) * np.exp2(np.arange(4) - 23.0)
        if kind[r] == 0:
            x[r, :, 0, :, 0] = rng.choice([-1.0, 1.0])
            x[r, :, 8] = digits
            x[r, :, 11, :, 0] = 2.0 ** -10
        if kind[r] == 1: x[r, :, 8] = digits * rng.choice([-1.0, 1.0], (8, C, 1))
        if kind[r] == 2:
            e = rng.integers(-1, 2, (8, C)) * least
            x[r, :, 8, :, 0] = 1.25 * e
            x[r, :, 9, :, 0] = -1.125 * e
            x[r, :, 13, :, 0] = rng.choice([-1.0, 1.0], (8, C)) * least
            for g in range(8): w[r, g, 13, 0, g, 12, 0] = 2.0 ** -8
        for g, j in zip(rng.permutation(8)[:4], [0, C - 1, int(rng.integers(C)), int(rng.integers(C))]): x[r, g, 0, j, 0] = 2.0 ** 29 * rng.choice([-1.0, 1.0])
        k = size[r] if kind[r] == 0 else least
        for h in range(0, 128, 16):
            u[r, h, h, 0] = k if kind[r] == 0 else 1.0
            if kind[r] == 0: u[r, h + 11, h, 0] = k
            if kind[r] < 2: u[r, h + 8, h] = k
            else:
                u[r, h + 8, h, 0] = k
                u[r, h + 9, h, 0] = 1.125 * k
                u[r, h + 12, h, 0] = k
    return {"x": x.reshape(N, 128, 4 * C).astype(BF), "u": u.reshape(N, 128, 512), "v": d["v"], **stored(*orders(rng)), **weights(rng, w)}
def setup_inputs_odd(rng):
    d = numbers_of(rng)
    x = (1.0 + (2 * rng.integers(0, 64, (N, 16, 8, C, 4)) + 1) * 2.0 ** -7) * np.exp2(-rng.integers(0, 7, (N, 16, 8, C, 4)).astype(np.float64)) * rng.choice([-1.0, 1.0], (N, 16, 8, C, 4))
    x[:, :, 0, :, 0] = 1.96875 * 2.0 ** 8 * rng.choice([-1.0, 1.0], (16, 1))
    u = d["u"].reshape(N, 16, 8, 128, 4)
    u[:, :, 0, ::16] = 0
    w = layers(rng, [0, 8])
    for g in range(8):
        for i in (0, 8): w[:, g, i, 0, g, i, 0] = -0.5
    return {"x": x.astype(np.float32).reshape(N, 128, 4 * C).astype(BF), "u": u.reshape(N, 128, 512), "v": d["v"], **stored(*orders(rng)), **weights(rng, w)}
def setup_inputs_ends(rng):
    d = numbers_of(rng)
    n, e, c = [rng.permutation(N) % 4 for _ in range(3)]
    low, tiny = 2.0 ** 29, 2.0 ** -30
    def small(*s): return (1 + 0.125 * rng.integers(0, 8, s)) * tiny
    x = np.zeros((N, 8, 16, C, 4))
    u = d["u"].astype(np.float32).reshape(N, 8, 16, 128, 4)
    v = d["v"].astype(np.float32)
    w = np.zeros((N, 128, 4, 128, 4), np.float32)
    i = np.arange(128)
    p, o = orders(rng)
    for r in range(N):
        h = rng.permutation(8)
        a = np.where(h < 2, 0.0, h % 2 * 2.0 - 1.0)[:, None]
        k = np.full(16, 4.0)
        k[15] = 0
        if n[r] < 2:
            x[r] = -(1 + 0.125 * rng.integers(0, 4, (8, 16, C, 4))) * low
            if n[r] == 1: x[r] *= rng.choice([-1.0, 1.0], (C, 1))
            x[r, :, 15] = 2.0 ** 16 * rng.choice([-1.0, 1.0], (8, C, 4))
            u[r, :, :, ::16] = a * 2.0 ** 30
            v[r] = rng.choice([-1.0, 1.0], (128, 512)) * (1 + 0.125 * rng.integers(4, 9, (128, 512))) * low
        elif n[r] == 2:
            x[r] = -small(8, 16, C, 4)
            u[r, :, :, ::16] = a * small(8, 16, 8, 4)
            u[r, :, 14:, ::16] = 0
            v[r] = rng.choice([-1.0, 1.0], (128, 512)) * small(128, 512)
            k[:] = 0
            k[14], k[15] = 2.0 ** -8, 2.0 ** 8
        else:
            x[r] = d["x"][r].astype(np.float32).reshape(8, 16, C, 4)[:, :, :1]
            u[r, :, :, ::16] *= np.abs(a).astype(np.float32)
        for b in range(4): w[r, i, b, i, b] = np.tile(k, 8)
        if e[r] < 3: p[r] = [np.arange(C), np.arange(C)[::-1], (np.arange(C) + 1) % C][e[r]]
        up = np.arange(8)[:, None]
        if c[r] < 3: o[r] = np.where([np.ones(C, bool), np.zeros(C, bool), rng.random(C) < 0.5][c[r]], up, 7 - up)
    return {"x": x.astype(np.float32).reshape(N, 128, 4 * C).astype(BF), "u": u.reshape(N, 128, 512).astype(BF), "v": v.astype(BF), **stored(p, o), **weights(rng, w.astype(BF))}
def setup_inputs_spread(rng):
    d = setup_inputs(rng)
    d["x"] = wide(rng, N, 128, 4 * C, cols=6)
    return d
def check_inputs(d):
    b = []
    for k in ("x", "u", "v"):
        a = np.abs(d[k].astype(np.float32))
        if not (np.isfinite(a).all() and ((a == 0) | (a >= 2.0 ** -30) & (a <= 2.0 ** 30)).all()): b.append("a value of " + k)
    none, least, most = [emit(mx_ref.quantize(np.full((128, 16), k, np.float32).astype(BF)))[1][0, 0] for k in (0.0, 2.0 ** -8, 2.0 ** 8)]
    for r in range(N):
        if not (np.sort(gentries(d["pg"][r]), axis=1) == np.arange(C)).all(): b.append("pg: a group's entries aren't all columns")
        if not (np.sort(gentries(d["og"][r]), axis=0) == np.arange(8)[:, None]).all(): b.append("og: a column's entries aren't all groups")
        if ((d["wc"][r] == 0x7F) | (d["wc"][r] == 0xFF)).any(): b.append("wc: a code that is no number")
        s = mx_ref.live(d["ws"][r])
        if ((s != none) & ((s < least) | (s > most))).any(): b.append("ws: a scale out of range")
        if (((d["wc"][r].reshape(16, 8, 512, 4) & 0x7F) != 0) & (s == none)[:, None, :, None]).any(): b.append("wc: a code other than zero under the scale of zeros")
    return b
def walk(p, o):
    a, at = np.arange(C), np.zeros((8, C), np.int64)
    for k in range(8):
        a = p[o[k], a]
        at[o[k], np.arange(C)] = a
    return at
def reference(x, u, v, pg, og, wc, ws):
    qu = [mx_ref.quantize(u[r]) for r in range(N)]
    lay = [pk(wc[r], ws[r]) for r in range(N)]
    p, o = [np.array(gentries(pg[r])) for r in range(N)], [np.array(gentries(og[r])) for r in range(N)]
    at = [walk(p[r], o[r]) for r in range(N)]
    now = [x[r] for r in range(N)]
    for t, step in enumerate(STEP):
        held, z = [], []
        for r in range(N):
            q = mx_ref.quantize(now[r])
            held.append(decode(q))
            s = mx_ref.matmul(qu[r], q)[::16]
            c = s[o[r], at[r][o[r], np.arange(C)]]
            for k in range(t % 2, 7, 2):
                turn = c[k] > c[k + 1]
                o[r][k], o[r][k + 1] = np.where(turn, o[r][k + 1], o[r][k]), np.where(turn, o[r][k], o[r][k + 1])
            at[r] = walk(p[r], o[r])
            z.append(mx_ref.quantize(gcols(held[r].astype(BF), at[r])))
        for r in range(N):
            e = np.take_along_axis(p[r], at[r], axis=1)
            now[r] = tile([held[r][:, b::4] + gpick(mx_ref.matmul(pick(lay[r], np.arange(128 * b, 128 * b + 128)), z[r ^ step]) * np.float32(0.03125), e) for b in range(4)])
    y, ol = np.zeros((N, 128, C), np.float32), np.zeros((N, 8, C), np.float32)
    oc, osc = np.zeros((N, 128, 4 * C), np.uint8), np.zeros((N, 16, C), np.uint8)
    for r in range(N):
        q = mx_ref.quantize(now[r])
        y[r] = mx_ref.matmul(mx_ref.quantize(v[r]), q)
        ol[r] = o[r]
        oc[r], osc[r] = emit(q)
    return {"y": y, "ol": ol, "oc": oc, "osc": osc}

@@ -1,0 +1,450 @@
+from concourse.mybir import dt, AluOpType, ActivationFunctionType
+
+COPY = ActivationFunctionType.Copy
+ADD, SUB, MUL, MAX, MIN = AluOpType.add, AluOpType.subtract, AluOpType.mult, AluOpType.max, AluOpType.min
+BIG = 1048576.0
+C = 320
+STEP = [1, 2, 4]
+CH = [(0, 192), (192, 320)]
+
+SCRATCH = {}
+
+
+def _d(name, cols, dtype, where="sbuf"):
+    SCRATCH[name] = (where, [128, cols], dtype)
+
+
+ALIAS = {}
+
+
+def _share(buf, dtype, *parts):
+    at = 0
+    for n, c in parts:
+        ALIAS[n] = (buf, at, c)
+        at += c + c % 2
+    _d(buf, at, dtype)
+
+
+_share("iv", "int32", ("pint", 1), ("lanei", 1), ("hi", 1), ("xi", 1), ("sxi", 1), ("sx7", 1), ("upi", 16), ("mi", 24), ("pi0", 24), ("pi1", 24), ("pi2", 24))
+_share("iw", "int32", ("ogr", 20), ("og7", 20), ("ls0", 24), ("ls1", 24), ("ls2", 24))
+_share("fv", "float32", ("lanef", 1), ("hf", 1), ("h8", 1), ("h2", 1), ("ux", 1), ("xf", 1), ("lan16", 1), ("eb", 4), ("ge20", 24), ("ge40", 24), ("ja", 48), ("jf", 48))
+_share("uv", "uint16", ("pgu", 20), ("ogu", 20), ("upu", 16), ("cl", 24), ("gw", 24))
+_d("pgi", 20, "int32")
+_d("ogi", 20, "int32")
+for _n, _c in (("i512", 512), ("i16", 384), ("i8", 320), ("w320", 8), ("wone", 8),
+               ("msk", 384), ("r16a", 384), ("r16", 384), ("r8a", 320), ("r8", 320), ("lab", 320), ("un", 384), ("ka", 384),
+               ("N", 384), ("K", 384), ("DN", 192), ("DK", 192), ("MN", 192), ("MK", 192), ("E", 192), ("CC", 192),
+               ("G", 48), ("SC", 48), ("VV", 384), ("SV", 320), ("VF", 384), ("SF", 384), ("ST", 2560), ("BG", 320), ("BS", 320),
+               ("rb0", 320), ("rb1", 320), ("rb2", 320), ("rb3", 320), ("lm", 384), ("o1", 384), ("o2", 192), ("o3", 96), ("o4", 48),
+               ("olf", 320), ("yb", 320)):
+    _d(_n, _c, "float32")
+for _n, _c in (("off", 32), ("fl0", 26), ("fl1", 26), ("fl2", 26), ("ol40", 40), ("ow", 20)):
+    _d(_n, _c, "uint16")
+for _t in range(3):
+    _d("ml%d" % _t, 40, "uint16")
+    _d("ll%d" % _t, 40, "uint16")
+    _d("al%d" % _t, 20, "uint16")
+    _d("pl%d" % _t, 20, "uint16")
+    _d("bl%d" % _t, 20, "uint16")
+    _d("fo%d" % _t, 1280, "bfloat16")
+    _d("fp%d" % _t, 1280, "bfloat16")
+    _d("zt%d" % _t, 1280, "bfloat16")
+    _d("zc%d" % _t, 320, "float8_e4m3fn_x4")
+    _d("zs%d" % _t, 320, "uint8")
+    _d("lc%d" % _t, 320, "float8_e4m3fn_x4")
+    _d("lp%d" % _t, 320, "uint8")
+for _t in range(4):
+    _d("xt%d" % _t, 1280, "bfloat16")
+    _d("qc%d" % _t, 320, "float8_e4m3fn_x4")
+    _d("qs%d" % _t, 320, "uint8")
+for _n, _c in (("i320", 320), ("P", 2560), ("ec", 2048), ("ut", 512), ("vt", 512)):
+    _d(_n, _c, "bfloat16")
+for _n, _c in (("eq", 512), ("wq", 512), ("uq", 128), ("uw", 256), ("vq", 128)):
+    _d(_n, _c, "float8_e4m3fn_x4")
+    _d(_n + "s", _c, "uint8")
+for _k in range(8):
+    _d("ps%d" % _k, 512, "float32", "psum")
+
+DMA_SEMS = ["dpg", "dog", "du", "dxa", "dxb", "dw", "dv", "dp", "own0", "own1", "own2", "par0", "par1", "par2", "do1", "do2", "dout"]
+SEMAPHORES = ["cv", "cs", "ct", "cg", "left", "rq0", "rq1", "rq2", "rl0", "rl1", "rl2"] + DMA_SEMS
+
+
+def slot(k):
+    return k // 2 + (4 if k % 2 else 0)
+
+
+def rank_program(g, core, T, topo):
+    rank = T.rank_of(core)
+    if rank is None:
+        return
+    queue = {"v": g.vector, "s": g.scalar, "t": g.tensor, "g": g, "y": g.sync}
+    total = {s: 0 for s in SEMAPHORES}
+    clock = {q: {} for q in queue}
+    wrote, read = {}, {}
+
+    def O(name, lo=0, hi=None, step=1):
+        if name in ALIAS:
+            name, at, n = ALIAS[name]
+            lo, hi = at + lo, at + (n if hi is None else hi)
+        hi = SCRATCH[name][1][1] if hi is None else hi
+        ap = T[name][:, lo:hi] if step == 1 else T[name][:, lo:hi:step]
+        return (ap, [(name, lo, hi, step, lo % step)])
+
+    def codes(o):
+        return (o[0].bitcast(dt.uint8), o[1])
+
+    def words(o):
+        return (o[0].bitcast(dt.uint32), o[1])
+
+    def by(win, off):
+        return (win[0].indirect(off[0]), win[1] + off[1])
+
+    def meet(a, b):
+        return a[1] < b[2] and b[1] < a[2] and not (a[3] == b[3] > 1 and a[4] != b[4])
+
+    def order(q, reads, writes, dma=False):
+        evs = []
+        writes = writes + [r for r in reads if r[0][:2] == "ps"]
+        for r in reads:
+            evs += [e for w, e in wrote.get(r[0], []) if meet(r, w)]
+        for r in writes:
+            evs += [e for w, e in wrote.get(r[0], []) if meet(r, w)]
+            evs += [e for w, e in read.get(r[0], []) if meet(r, w) and (dma or e[3] != q)]
+        want = {}
+        for sem, val, snap, who in evs:
+            if clock[q].get(sem, 0) < val and want.get(sem, (0,))[0] < val:
+                want[sem] = (val, snap)
+        for sem in list(want):
+            if any(o != sem and want[o][1].get(sem, 0) >= want[sem][0] for o in want):
+                del want[sem]
+        for sem, (val, snap) in want.items():
+            queue[q].wait_ge(T.sem[sem], val)
+            for s2, v2 in list(snap.items()) + [(sem, val)]:
+                clock[q][s2] = max(clock[q].get(s2, 0), v2)
+
+    def note(reads, writes, ev):
+        for r in reads:
+            read.setdefault(r[0], []).append((r, ev))
+        for w in writes:
+            old = wrote.get(w[0], [])
+            wrote[w[0]] = [(o, e) for o, e in old if not (w[3] == 1 and w[1] <= o[1] and o[2] <= w[2])] + [(w, ev)]
+            if w[0] in read:
+                read[w[0]] = [(o, e) for o, e in read[w[0]] if not (w[3] == 1 and w[1] <= o[1] and o[2] <= w[2])]
+
+    def run(q, outs, ins, call):
+        reads = [r for o in ins for r in o[1]]
+        writes = [r for o in outs for r in o[1]]
+        order(q, reads, writes)
+        sem = "c" + q
+        total[sem] += 1
+        snap = dict(clock[q])
+        call().then_inc(T.sem[sem], 1)
+        note(reads, writes, (sem, total[sem], snap, q))
+
+    def dmas(sem, items):
+        snap, acc = {}, []
+        for q, out, in_, writes, reads in items:
+            order(q, reads, writes, True)
+            queue[q].dma_start(out, in_).then_inc(T.sem[sem], 16)
+            total[sem] += 16
+            for s2, v2 in clock[q].items():
+                snap[s2] = max(snap.get(s2, 0), v2)
+            acc.append((reads, writes))
+        for reads, writes in acc:
+            note(reads, writes, (sem, total[sem], snap, "dma"))
+
+    def arrives(sem, val, outs):
+        total[sem] += val
+        note([], [r for o in outs for r in o[1]], (sem, val, {}, "far"))
+
+    def copy(out, in_, q="v"):
+        if q == "v":
+            run(q, [out], [in_], lambda: g.vector.tensor_copy(out[0], in_[0]))
+        else:
+            run(q, [out], [in_], lambda: g.scalar.activation(out[0], in_[0], COPY))
+
+    def tt(out, a, b, op):
+        run("v", [out], [a, b], lambda: g.vector.tensor_tensor(out[0], a[0], b[0], op))
+
+    def ts(out, a, s1, s2, op0, op1=None):
+        ins = [a] + [s for s in (s1, s2) if isinstance(s, tuple)]
+        v1 = s1[0] if isinstance(s1, tuple) else s1
+        v2 = s2[0] if isinstance(s2, tuple) else s2
+        if op1 is None:
+            run("v", [out], ins, lambda: g.vector.tensor_scalar(out[0], a[0], v1, None, op0))
+        else:
+            run("v", [out], ins, lambda: g.vector.tensor_scalar(out[0], a[0], v1, v2, op0, op1))
+
+    def scan(out, reset, data):
+        run("v", [out], [reset, data], lambda: g.vector.tensor_tensor_scan(out[0], reset[0], data[0], -2.0 * BIG, MIN, MAX))
+
+    def iota(out, pattern, base, mul):
+        kw = {} if SCRATCH[out[1][0][0]][2] == "int32" else {"allow_small_or_imprecise_dtypes": True}
+        run("g", [out], [], lambda: g.iota(out[0], pattern, base, mul, **kw))
+
+    def quant(cn, sn, xn, lo, hi):
+        q, s, x = O(cn, lo, hi), O(sn, lo, hi), O(xn, 4 * lo, 4 * hi)
+        run("v", [q, s], [x], lambda: g.vector.quantize_mx(q[0], s[0], x[0]))
+
+    bank = [0]
+
+    def mx(an, alo, bn, lo, hi, bsn=None, asn=None):
+        k = bank[0] % 8
+        bank[0] += 1
+        out = O("ps%d" % k, 0, hi - lo)
+        full = (out[0], [("ps%d" % k, 0, 512, 1, 0)])
+        a, s = O(an, alo, alo + 128), O(asn or an + "s", alo, alo + 128)
+        b, p = O(bn, lo, hi), O(bsn, lo, hi)
+        run("t", [full], [a, s, b, p], lambda: g.tensor.matmul_mx(out[0], a[0], s[0], b[0], p[0], True, True))
+        return full
+
+    def load(q, name, src, lo, hi, fn=None):
+        o = O(name, lo, hi)
+        return (q, (fn(o) if fn else o)[0], src, o[1], [])
+
+    dmas("dpg", [load("y", "pgi", T.pg[:], 0, 20)])
+    dmas("du", [load("s", "ut", T.u[:], 0, 512)])
+    dmas("dxa", [load("y", "xt0", T.x[:, 0:768], 0, 768)])
+    dmas("dxb", [load("y", "xt0", T.x[:, 768:1280], 768, 1280)])
+    dmas("dog", [("s" if d else "y", T.ogi[2 * k + d:128:16, 0:20], T.og[16 * k + d:16 * k + 16:2, 0:20], [("ogi", 0, 20, 1, 0)], [])
+                 for k in range(8) for d in range(2)])
+
+    iota(O("pint"), [[1, 1]], 0, 1)
+    iota(O("i320"), [[1, 320]], -160, 0)
+    iota(O("upi"), [[0, 2], [16, 8]], 0, 0)
+    iota(O("w320"), [[320, 8]], 160, 0)
+    iota(O("mi"), [[0, 8], [16, 3]], 0, 0)
+    iota(O("pi0"), [[2, 2], [4, 4], [256, 3]], 0, 0)
+    iota(O("i16"), [[0, 24], [1, 16]], 0, 0)
+    iota(O("ja", 0, 40), [[1, 2], [16, 20]], 0, 0)
+    iota(O("ja", 40, 48), [[16, 8]], 0, 0)
+    iota(O("eb"), [[1, 4]], 0, 4)
+    iota(O("i512"), [[1, 512]], 0, 0)
+    iota(O("i8"), [[0, 40], [1, 8]], 0, 0)
+
+    AND, SHR, EQ, GE, GT, LT = (AluOpType.bitwise_and, AluOpType.arith_shift_right, AluOpType.is_equal, AluOpType.is_ge,
+                                AluOpType.is_gt, AluOpType.is_lt)
+    ts(O("lanei"), O("pint"), 15, None, AND)
+    ts(O("hi"), O("pint"), 4, None, SHR)
+    ts(O("xi"), O("pint"), 7, None, AND)
+    copy(O("lanef"), O("lanei"))
+    copy(O("hf"), O("hi"))
+    ts(O("h8"), O("hf"), 8.0, None, ADD)
+    copy(O("upu"), O("upi"))
+    copy(O("pgu"), O("pgi"))
+    copy(O("P", 0, 320), by(O("i320"), O("pgu")))
+    items = []
+    for s in range(1, 8):
+        w = [("P", 320 * s, 320 * s + 320, 1, 0)]
+        r = [("P", 0, 320, 1, 0)]
+        q = "y" if s % 2 else "s"
+        items.append((q, T.P[16 * s:128, 320 * s:320 * s + 320], T.P[0:128 - 16 * s, 0:320], w, r))
+        items.append((q, T.P[0:16 * s, 320 * s:320 * s + 320], T.P[128 - 16 * s:128, 0:320], w, r))
+    dmas("dp", items)
+    dmas("dw", [("y", codes(O("wq"))[0], T.wc[:], O("wq")[1], []), ("y", O("wqs")[0], T.ws[:], O("wqs")[1], [])])
+    dmas("dv", [load("y", "vt", T.v[:], 0, 512)])
+
+    quant("uq", "uqs", "ut", 0, 128)
+    copy(words(O("uw")), by(words(O("uq")), O("upu")))
+    copy(O("uws"), by(O("uqs"), O("upu")), "s")
+    for lo, hi in CH:
+        quant("qc0", "qs0", "xt0", lo, hi)
+
+    def scores(t, piece):
+        lo, hi = CH[piece]
+        for s in range(8):
+            p = mx("uw", 16 * (8 - s), "qc%d" % t, lo, hi, "qs%d" % t)
+            q = "v" if t and piece and s % 2 else "s"
+            copy(O("ST", 320 * s + lo, 320 * s + hi), (p[0], p[1]), q)
+
+    partner = [T.cores[rank ^ s] for s in STEP]
+
+    def send(t, out, in_, sem):
+        rid, pid, _s = topo.addr(partner[t])
+        eng = topo.engines(core, partner[t])[::2]
+        order("g", in_[1], [])
+        g.remote_dma(out[0], in_[0], T.sem[sem], T.sem.left, pid=pid, routing_id=rid, dma_engine_mask=sum(1 << e for e in eng))
+        total["left"] += len(eng)
+        return len(eng)
+
+    def send_state(t):
+        n = send(t, codes(O("lc%d" % t)), codes(O("qc%d" % t)), "rq%d" % t)
+        n += send(t, O("lp%d" % t), O("qs%d" % t), "rq%d" % t)
+        arrives("rq%d" % t, n, [O("lc%d" % t), O("lp%d" % t)])
+
+    send_state(0)
+    scores(0, 0)
+    scores(0, 1)
+
+    ts(O("ogr"), O("ogi"), -1.0, O("h8"), MUL, ADD)
+    ts(O("og7"), O("ogr"), 7, None, AND)
+    copy(O("ogu"), O("og7"))
+    copy(O("lab"), by(O("w320"), O("ogu")))
+    ts(O("lan16"), O("lanef"), 16.0, None, MUL)
+    ts(O("pi1"), O("mi"), O("lanef"), None, ADD)
+    ts(O("ge20"), O("pi1"), 20.0, -319.0, GE, MUL)
+    ts(O("ge40"), O("pi1"), 40.0, -321.0, GE, MUL)
+    tt(O("ge20"), O("ge20"), O("ge40"), ADD)
+    ts(O("pi2"), O("pi0"), O("lan16"), None, ADD)
+    tt(O("pi2"), O("pi2"), O("ge20"), ADD)
+    copy(O("cl"), O("pi2"))
+    ts(O("msk"), O("i16"), O("lanef"), BIG, EQ, MUL)
+    ts(O("msk"), O("msk"), -BIG, None, ADD)
+    ts(O("r16a"), O("i16"), 0.5, 4.0 * BIG, GT, MUL)
+    ts(O("r16"), O("r16a"), -2.0 * BIG, None, ADD)
+    tt(O("N"), by(O("lab"), O("cl")), O("msk"), ADD)
+    ts(O("h2"), O("hf"), 2.0, -160.0, MUL, ADD)
+    ts(O("jf"), O("ja"), O("h2"), None, ADD)
+
+    def P_by(k):
+        return by(O("P"), O("off", 4 * k, 4 * k + 3))
+
+    def place(name, k):
+        return O(name, 48 * slot(k), 48 * slot(k) + 48)
+
+    def walk(beside):
+        tt(O("G"), place("N", 0), O("jf"), ADD)
+        for k in range(8):
+            scan(O("SC"), O("r16", 0, 48), O("G"))
+            copy(O("off", 4 * k, 4 * k + 3), O("SC", 15, 48, 16))
+            if k < 7:
+                tt(O("G"), P_by(k), place("N", k + 1), ADD)
+            for call in beside[k]:
+                call()
+
+    def score_places(k):
+        tt(place("VF", k), P_by(k), place("N", k), ADD)
+
+    def score_list(t):
+        scan(O("SF"), O("r16"), O("VF"))
+        if t == 1:
+            copy(O("fl1", 1, 13), O("SF", 15, 192, 16))
+            copy(O("fl1", 14, 26), O("SF", 207, 384, 16))
+        else:
+            copy(O("fl%d" % t, 0, 24), O("SF", 15, 384, 16))
+
+    for b in range(4):
+        ts(O("ec", 512 * b, 512 * b + 512), O("i512"), O("eb", b, b + 1), None, EQ)
+    quant("eq", "eqs", "ec", 0, 512)
+
+    walk([[lambda k=k: score_places(k)] for k in range(8)])
+    score_list(0)
+
+    tt(O("sxi"), O("hi"), O("xi"), SUB)
+    ts(O("sx7"), O("sxi"), 7, None, AND)
+    ts(O("ux"), O("sx7"), 320.0, 160.0, MUL, ADD)
+    copy(O("un"), by(O("lab"), O("cl")))
+    ts(O("ka"), O("un"), O("ux"), BIG, EQ, MUL)
+    ts(O("K"), O("ka"), 160.0 - BIG, None, ADD)
+    ts(O("r8a"), O("i8"), 0.5, 4.0 * BIG, GT, MUL)
+    ts(O("r8"), O("r8a"), -2.0 * BIG, None, ADD)
+
+    def sides(t):
+        return ((192, 336), (48, 192)) if t == 1 else ((0, 192), (192, 384))
+
+    def differences(t):
+        a, b = sides(t)
+        n = a[1] - a[0]
+        tt(O("DN", 0, n), O("N", *b), O("N", *a), SUB)
+        tt(O("DK", 0, n), O("K", *b), O("K", *a), SUB)
+
+    def exchange(t, name, diff, tmp):
+        a, b = sides(t)
+        n = a[1] - a[0]
+        return [lambda: tt(O(tmp, 0, n), O(diff, 0, n), O("CC", 0, n), MUL),
+                lambda: tt(O(name, *a), O(name, *a), O(tmp, 0, n), ADD),
+                lambda: tt(O(name, *b), O(name, *b), O(tmp, 0, n), SUB)]
+
+    def pick(k):
+        tt(O("VV", k, 384, 8), P_by(k), place("K", k), ADD)
+
+    def spread(sem, out, in_, qs):
+        dmas(sem, [(qs[i % len(qs)], T[out][16 * i:16 * i + 16, 0:20], T[in_][i:128:16, 0:40], [(out, 0, 20, 1, 0)], [(in_, 0, 40, 1, 0)])
+                   for i in range(8)])
+
+    def unpack(t, name, cn, sn):
+        for b in range(4):
+            p = mx("eq", 128 * b, cn, 0, 320, sn)
+            copy(O("%s%d" % (name, t), 320 * b, 320 * b + 320), p, "s")
+
+    differences(0)
+    for t in range(3):
+        n = sides(t)[0][1] - sides(t)[0][0]
+        unpack(t, "fo", "qc%d" % t, "qs%d" % t)
+        unpack(t, "fp", "lc%d" % t, "lp%d" % t)
+        first, second = ((14, 23), (4, 13)) if t == 1 else ((0, 12), (12, 24))
+        copy(O("E", 0, n), by(O("ST"), O("fl%d" % t, *first)))
+        tt(O("CC", 0, n), by(O("ST"), O("fl%d" % t, *second)), O("E", 0, n), LT)
+        for call in exchange(t, "N", "DN", "MN"):
+            call()
+        later = exchange(t, "K", "DK", "MK")
+        p = [lambda k=k: pick(k) for k in range(8)]
+        walk([[later[0]], [later[1]], [later[2]], p[0:2], p[2:4], p[4:5], p[5:7], p[7:]])
+        scan(O("SV"), O("r8"), O("VV", 0, 320))
+        copy(O("ml%d" % t), O("SV", 7, 320, 8))
+        k = send(t, O("ll%d" % t), O("ml%d" % t), "rl%d" % t)
+        arrives("rl%d" % t, k, [O("ll%d" % t)])
+        spread("own%d" % t, "al%d" % t, "ml%d" % t, "y")
+        if t < 2:
+            for k in range(8):
+                score_places(k)
+            score_list(t + 1)
+            differences(t + 1)
+        else:
+            scan(O("SF"), O("r16"), O("N"))
+            ts(O("ls0"), O("SF", 15, 384, 16), -160.0, 1.0 / 320.0, ADD, MUL)
+            ts(O("ls1"), O("ls0"), -1.0, O("h8"), MUL, ADD)
+            ts(O("ls2"), O("ls1"), 7, None, AND)
+            copy(O("gw"), O("ls2"))
+            iota(O("wone"), [[1, 8]], 0, 0)
+            iota(O("lm"), [[1, 2], [2, 4], [0, 48]], 0, 0)
+            copy(O("xf"), O("xi"))
+            ts(O("lm"), O("lm"), O("xf"), None, EQ)
+            tt(O("o1"), by(O("wone"), O("gw")), O("lm"), MUL)
+            tt(O("o2"), O("o1", 0, 192), O("o1", 192, 384), ADD)
+            tt(O("o3"), O("o2", 0, 96), O("o2", 96, 192), ADD)
+            tt(O("o4"), O("o3", 0, 48), O("o3", 48, 96), ADD)
+            copy(O("ol40"), O("o4", 0, 40))
+            spread("do1", "ow", "ol40", "y")
+        tt(O("BG"), by(O("P", 0, 320), O("al%d" % t)), O("msk", 0, 320), ADD)
+        scan(O("BS"), O("r16", 0, 320), O("BG"))
+        ts(O("bl%d" % t), O("BS", 15, 320, 16), 160.0, None, ADD)
+        spread("par%d" % t, "pl%d" % t, "ll%d" % t, "ys")
+        for lo, hi in CH:
+            off = O("pl%d" % t, lo // 16, hi // 16)
+            for b in range(4):
+                copy(O("zt%d" % t, 4 * lo + b, 4 * hi, 4), by(O("fp%d" % t, 320 * b, 320 * b + 320), off), "v" if b < 2 else "s")
+            quant("zc%d" % t, "zs%d" % t, "zt%d" % t, lo, hi)
+        for lo, hi in CH:
+            for b in range(4):
+                p = mx("wq", 128 * b, "zc%d" % t, lo, hi, "zs%d" % t)
+                o = O("rb%d" % b, lo, hi)
+                run("s", [o], [p], lambda o=o, p=p: g.scalar.activation(o[0], p[0], COPY, scale=0.03125))
+        for i, (lo, hi) in enumerate(CH):
+            off = O("bl%d" % t, lo // 16, hi // 16)
+            for b in range(4):
+                tt(O("xt%d" % (t + 1), 4 * lo + b, 4 * hi, 4), by(O("rb%d" % b), off), O("fo%d" % t, 320 * b + lo, 320 * b + hi), ADD)
+            quant("qc%d" % (t + 1), "qs%d" % (t + 1), "xt%d" % (t + 1), lo, hi)
+            if t < 2 and i == 0:
+                scores(t + 1, 0)
+        if t < 2:
+            send_state(t + 1)
+            scores(t + 1, 1)
+        else:
+            copy(O("olf"), by(O("wone"), O("ow")))
+            quant("vq", "vqs", "vt", 0, 128)
+    outs = [("y", T.ol[:], T.olf[0:128:16, 0:320], [], O("olf")[1])]
+    for lo, hi in CH:
+        o = O("qc3", lo, hi)
+        outs.append(("y", T.oc[:, 4 * lo:4 * hi], codes(o)[0], [], o[1]))
+    for k in range(4):
+        outs.append(("y", T.osc[4 * k:4 * k + 4, 0:320], T.qs3[32 * k:32 * k + 4, 0:320], [], O("qs3")[1]))
+    for lo, hi in CH:
+        p = mx("vq", 0, "qc3", lo, hi, "qs3")
+        o = O("yb", lo, hi)
+        copy(o, p, "s" if lo else "v")
+        outs.append(("s", T.y[:, lo:hi], o[0], [], o[1]))
+    dmas("dout", outs)
+    for s in SEMAPHORES:
+        if total[s]:
+            g.wait_ge(T.sem[s], total[s])

@@ -27,13 +27,13 @@ def _share(buf, dtype, *parts):
 
 _share("iv", "int32", ("pint", 1), ("lanei", 1), ("hi", 1), ("xi", 1), ("sxi", 1), ("sx7", 1), ("upi", 16), ("mi", 24), ("pi0", 24), ("pi1", 24), ("pi2", 24))
 _share("iw", "int32", ("ogr", 20), ("og7", 20), ("ls0", 24), ("ls1", 24), ("ls2", 24))
-_share("fv", "float32", ("lanef", 1), ("hf", 1), ("h8", 1), ("h2", 1), ("ux", 1), ("xf", 1), ("lan16", 1), ("eb", 4), ("ge20", 24), ("ge40", 24), ("ja", 48), ("jf", 48))
+_share("fv", "float32", ("lanef", 1), ("hf", 1), ("h8", 1), ("h2", 1), ("ux", 1), ("xf", 1), ("lan16", 1), ("lanem", 1), ("ge20", 24), ("ge40", 24), ("ja", 48), ("jf", 48))
 _share("uv", "uint16", ("pgu", 20), ("ogu", 20), ("upu", 16), ("cl", 24), ("gw", 24))
 _d("pgi", 20, "int32")
 _d("ogi", 20, "int32")
-for _n, _c in (("i512", 512), ("i16", 384), ("i8", 320), ("w320", 8), ("wone", 8),
-               ("msk", 384), ("r16a", 384), ("r16", 384), ("r8a", 320), ("r8", 320), ("lab", 320), ("un", 384), ("ka", 384),
-               ("N", 384), ("K", 384), ("DN", 192), ("DK", 192), ("MN", 192), ("MK", 192), ("E", 192), ("CC", 192),
+for _n, _c in (("i16", 384), ("i8", 320), ("w320", 8), ("wone", 8),
+               ("msk", 384), ("r16", 384), ("r8", 320), ("lab", 320),
+               ("N", 384), ("K", 384), ("DN", 192), ("KA", 192), ("KB", 192), ("KC", 192), ("MN", 192), ("E", 192), ("CC", 192),
                ("G", 48), ("SC", 48), ("VV", 384), ("SV", 320), ("VF", 384), ("SF", 384), ("ST", 2560), ("BG", 320), ("BS", 320),
                ("rb0", 320), ("rb1", 320), ("rb2", 320), ("rb3", 320), ("lm", 384), ("o1", 384), ("o2", 192), ("o3", 96), ("o4", 48),
                ("olf", 320), ("yb", 320)):
@@ -57,7 +57,7 @@ for _t in range(4):
     _d("xt%d" % _t, 1280, "bfloat16")
     _d("qc%d" % _t, 320, "float8_e4m3fn_x4")
     _d("qs%d" % _t, 320, "uint8")
-for _n, _c in (("i320", 320), ("P", 2560), ("ec", 2048), ("ut", 512), ("vt", 512)):
+for _n, _c in (("i320", 320), ("P", 2560), ("ones", 512), ("ec", 2048), ("ut", 512), ("vt", 512)):
     _d(_n, _c, "bfloat16")
 for _n, _c in (("eq", 512), ("wq", 512), ("uq", 128), ("uw", 256), ("vq", 128)):
     _d(_n, _c, "float8_e4m3fn_x4")
@@ -203,34 +203,48 @@ def rank_program(g, core, T, topo):
         return (q, (fn(o) if fn else o)[0], src, o[1], [])
 
     dmas("dpg", [load("y", "pgi", T.pg[:], 0, 20)])
+    dmas("dog", [("s" if d else "y", T.ogi[2 * k + d:128:16, 0:20], T.og[16 * k + d:16 * k + 16:2, 0:20], [("ogi", 0, 20, 1, 0)], [])
+                 for k in range(8) for d in range(2)])
     dmas("du", [load("s", "ut", T.u[:], 0, 512)])
     dmas("dxa", [load("y", "xt0", T.x[:, 0:768], 0, 768)])
     dmas("dxb", [load("y", "xt0", T.x[:, 768:1280], 768, 1280)])
-    dmas("dog", [("s" if d else "y", T.ogi[2 * k + d:128:16, 0:20], T.og[16 * k + d:16 * k + 16:2, 0:20], [("ogi", 0, 20, 1, 0)], [])
-                 for k in range(8) for d in range(2)])
+
+    AND, SHR, EQ, NE, GE, LT = (AluOpType.bitwise_and, AluOpType.arith_shift_right, AluOpType.is_equal, AluOpType.not_equal,
+                                AluOpType.is_ge, AluOpType.is_lt)
+
+    def select(out, in_, pattern, fill, base=0, mul=0):
+        run("g", [out], [in_], lambda: g.affine_select(out[0], in_[0], pattern, EQ, fill, base, mul))
 
     iota(O("pint"), [[1, 1]], 0, 1)
-    iota(O("i320"), [[1, 320]], -160, 0)
-    iota(O("upi"), [[0, 2], [16, 8]], 0, 0)
-    iota(O("w320"), [[320, 8]], 160, 0)
     iota(O("mi"), [[0, 8], [16, 3]], 0, 0)
     iota(O("pi0"), [[2, 2], [4, 4], [256, 3]], 0, 0)
-    iota(O("i16"), [[0, 24], [1, 16]], 0, 0)
+    iota(O("i320"), [[1, 320]], -160, 0)
     iota(O("ja", 0, 40), [[1, 2], [16, 20]], 0, 0)
     iota(O("ja", 40, 48), [[16, 8]], 0, 0)
-    iota(O("eb"), [[1, 4]], 0, 4)
-    iota(O("i512"), [[1, 512]], 0, 0)
-    iota(O("i8"), [[0, 40], [1, 8]], 0, 0)
+    iota(O("w320"), [[320, 8]], 160, 0)
+    iota(O("upi"), [[0, 2], [16, 8]], 0, 0)
+    iota(O("i16"), [[0, 24], [1, 16]], -2097152, 0)
+    select(O("r16"), O("i16"), [[0, 24], [1, 16]], 2.0 * BIG)
+    for b in range(4):
+        if b == 0:
+            run("v", [O("ones")], [], lambda: g.vector.memset(O("ones")[0], 1.0))
+        select(O("ec", 512 * b, 512 * b + 512), O("ones"), [[-1, 512]], 0.0, b, 4)
 
-    AND, SHR, EQ, GE, GT, LT = (AluOpType.bitwise_and, AluOpType.arith_shift_right, AluOpType.is_equal, AluOpType.is_ge,
-                                AluOpType.is_gt, AluOpType.is_lt)
     ts(O("lanei"), O("pint"), 15, None, AND)
     ts(O("hi"), O("pint"), 4, None, SHR)
     ts(O("xi"), O("pint"), 7, None, AND)
     copy(O("lanef"), O("lanei"))
     copy(O("hf"), O("hi"))
     ts(O("h8"), O("hf"), 8.0, None, ADD)
-    copy(O("upu"), O("upi"))
+    ts(O("lan16"), O("lanef"), 16.0, None, MUL)
+    ts(O("lanem"), O("lanef"), -2.0 * BIG, None, ADD)
+    ts(O("pi1"), O("mi"), O("lanef"), None, ADD)
+    ts(O("ge20"), O("pi1"), 20.0, -319.0, GE, MUL)
+    ts(O("ge40"), O("pi1"), 40.0, -321.0, GE, MUL)
+    tt(O("ge20"), O("ge20"), O("ge40"), ADD)
+    ts(O("pi2"), O("pi0"), O("lan16"), None, ADD)
+    tt(O("pi2"), O("pi2"), O("ge20"), ADD)
+    copy(O("cl"), O("pi2"))
     copy(O("pgu"), O("pgi"))
     copy(O("P", 0, 320), by(O("i320"), O("pgu")))
     items = []
@@ -244,6 +258,16 @@ def rank_program(g, core, T, topo):
     dmas("dw", [("y", codes(O("wq"))[0], T.wc[:], O("wq")[1], []), ("y", O("wqs")[0], T.ws[:], O("wqs")[1], [])])
     dmas("dv", [load("y", "vt", T.v[:], 0, 512)])
 
+    ts(O("ogr"), O("ogi"), -1.0, O("h8"), MUL, ADD)
+    ts(O("og7"), O("ogr"), 7, None, AND)
+    copy(O("ogu"), O("og7"))
+    copy(O("lab"), by(O("w320"), O("ogu")))
+    ts(O("h2"), O("hf"), 2.0, -160.0, MUL, ADD)
+    ts(O("jf"), O("ja"), O("h2"), None, ADD)
+    ts(O("msk"), O("i16"), O("lanem"), -BIG, NE, MUL)
+    tt(O("N"), by(O("lab"), O("cl")), O("msk"), ADD)
+
+    copy(O("upu"), O("upi"))
     quant("uq", "uqs", "ut", 0, 128)
     copy(words(O("uw")), by(words(O("uq")), O("upu")))
     copy(O("uws"), by(O("uqs"), O("upu")), "s")
@@ -276,26 +300,6 @@ def rank_program(g, core, T, topo):
     scores(0, 0)
     scores(0, 1)
 
-    ts(O("ogr"), O("ogi"), -1.0, O("h8"), MUL, ADD)
-    ts(O("og7"), O("ogr"), 7, None, AND)
-    copy(O("ogu"), O("og7"))
-    copy(O("lab"), by(O("w320"), O("ogu")))
-    ts(O("lan16"), O("lanef"), 16.0, None, MUL)
-    ts(O("pi1"), O("mi"), O("lanef"), None, ADD)
-    ts(O("ge20"), O("pi1"), 20.0, -319.0, GE, MUL)
-    ts(O("ge40"), O("pi1"), 40.0, -321.0, GE, MUL)
-    tt(O("ge20"), O("ge20"), O("ge40"), ADD)
-    ts(O("pi2"), O("pi0"), O("lan16"), None, ADD)
-    tt(O("pi2"), O("pi2"), O("ge20"), ADD)
-    copy(O("cl"), O("pi2"))
-    ts(O("msk"), O("i16"), O("lanef"), BIG, EQ, MUL)
-    ts(O("msk"), O("msk"), -BIG, None, ADD)
-    ts(O("r16a"), O("i16"), 0.5, 4.0 * BIG, GT, MUL)
-    ts(O("r16"), O("r16a"), -2.0 * BIG, None, ADD)
-    tt(O("N"), by(O("lab"), O("cl")), O("msk"), ADD)
-    ts(O("h2"), O("hf"), 2.0, -160.0, MUL, ADD)
-    ts(O("jf"), O("ja"), O("h2"), None, ADD)
-
     def P_by(k):
         return by(O("P"), O("off", 4 * k, 4 * k + 3))
 
@@ -323,21 +327,18 @@ def rank_program(g, core, T, topo):
         else:
             copy(O("fl%d" % t, 0, 24), O("SF", 15, 384, 16))
 
-    for b in range(4):
-        ts(O("ec", 512 * b, 512 * b + 512), O("i512"), O("eb", b, b + 1), None, EQ)
-    quant("eq", "eqs", "ec", 0, 512)
-
     walk([[lambda k=k: score_places(k)] for k in range(8)])
     score_list(0)
+    quant("eq", "eqs", "ec", 0, 512)
+    iota(O("i8"), [[0, 40], [1, 8]], 0, 0)
+    select(O("r8"), O("i8"), [[0, 40], [1, 8]], 1.0)
+    iota(O("wone"), [[1, 8]], 0, 0)
+    iota(O("lm"), [[1, 2], [2, 4], [0, 48]], 0, 0)
 
     tt(O("sxi"), O("hi"), O("xi"), SUB)
     ts(O("sx7"), O("sxi"), 7, None, AND)
     ts(O("ux"), O("sx7"), 320.0, 160.0, MUL, ADD)
-    copy(O("un"), by(O("lab"), O("cl")))
-    ts(O("ka"), O("un"), O("ux"), BIG, EQ, MUL)
-    ts(O("K"), O("ka"), 160.0 - BIG, None, ADD)
-    ts(O("r8a"), O("i8"), 0.5, 4.0 * BIG, GT, MUL)
-    ts(O("r8"), O("r8a"), -2.0 * BIG, None, ADD)
+    ts(O("K"), by(O("lab"), O("cl")), O("ux"), None, EQ)
 
     def sides(t):
         return ((192, 336), (48, 192)) if t == 1 else ((0, 192), (192, 384))
@@ -346,17 +347,21 @@ def rank_program(g, core, T, topo):
         a, b = sides(t)
         n = a[1] - a[0]
         tt(O("DN", 0, n), O("N", *b), O("N", *a), SUB)
-        tt(O("DK", 0, n), O("K", *b), O("K", *a), SUB)
+        ts(O("KC", 0, n), O("K", *b), 2.0, -1.0, MUL, ADD)
+        tt(O("KA", 0, n), O("KC", 0, n), O("K", *a), ADD)
+        ts(O("KB", 0, n), O("KA", 0, n), -1.0, 1.0, MUL, ADD)
 
-    def exchange(t, name, diff, tmp):
+    def exchange(t):
         a, b = sides(t)
         n = a[1] - a[0]
-        return [lambda: tt(O(tmp, 0, n), O(diff, 0, n), O("CC", 0, n), MUL),
-                lambda: tt(O(name, *a), O(name, *a), O(tmp, 0, n), ADD),
-                lambda: tt(O(name, *b), O(name, *b), O(tmp, 0, n), SUB)]
+        return [lambda: tt(O("MN", 0, n), O("DN", 0, n), O("CC", 0, n), MUL),
+                lambda: tt(O("N", *a), O("N", *a), O("MN", 0, n), ADD),
+                lambda: tt(O("N", *b), O("N", *b), O("MN", 0, n), SUB),
+                lambda: tt(O("K", *a), O("KA", 0, n), O("CC", 0, n), EQ),
+                lambda: tt(O("K", *b), O("KB", 0, n), O("CC", 0, n), EQ)]
 
     def pick(k):
-        tt(O("VV", k, 384, 8), P_by(k), place("K", k), ADD)
+        tt(O("VV", k, 384, 8), P_by(k), place("K", k), MUL)
 
     def spread(sem, out, in_, qs):
         dmas(sem, [(qs[i % len(qs)], T[out][16 * i:16 * i + 16, 0:20], T[in_][i:128:16, 0:40], [(out, 0, 20, 1, 0)], [(in_, 0, 40, 1, 0)])
@@ -375,13 +380,14 @@ def rank_program(g, core, T, topo):
         first, second = ((14, 23), (4, 13)) if t == 1 else ((0, 12), (12, 24))
         copy(O("E", 0, n), by(O("ST"), O("fl%d" % t, *first)))
         tt(O("CC", 0, n), by(O("ST"), O("fl%d" % t, *second)), O("E", 0, n), LT)
-        for call in exchange(t, "N", "DN", "MN"):
+        ex = exchange(t)
+        for call in ex[:3]:
             call()
-        later = exchange(t, "K", "DK", "MK")
         p = [lambda k=k: pick(k) for k in range(8)]
-        walk([[later[0]], [later[1]], [later[2]], p[0:2], p[2:4], p[4:5], p[5:7], p[7:]])
-        scan(O("SV"), O("r8"), O("VV", 0, 320))
-        copy(O("ml%d" % t), O("SV", 7, 320, 8))
+        walk([ex[3:4], ex[4:5], p[0:2], p[2:3], p[3:4], p[4:6], p[6:7], p[7:]])
+        run("v", [O("SV")], [O("r8"), O("VV", 0, 320)],
+            lambda: g.vector.tensor_tensor_scan(O("SV")[0], O("r8")[0], O("VV", 0, 320)[0], 0.0, MUL, ADD))
+        ts(O("ml%d" % t), O("SV", 7, 320, 8), 160.0, None, ADD)
         k = send(t, O("ll%d" % t), O("ml%d" % t), "rl%d" % t)
         arrives("rl%d" % t, k, [O("ll%d" % t)])
         spread("own%d" % t, "al%d" % t, "ml%d" % t, "y")
@@ -390,26 +396,27 @@ def rank_program(g, core, T, topo):
                 score_places(k)
             score_list(t + 1)
             differences(t + 1)
+            if t == 0:
+                quant("vq", "vqs", "vt", 0, 128)
+                copy(O("xf"), O("xi"))
+                ts(O("lm"), O("lm"), O("xf"), None, EQ)
         else:
             scan(O("SF"), O("r16"), O("N"))
             ts(O("ls0"), O("SF", 15, 384, 16), -160.0, 1.0 / 320.0, ADD, MUL)
             ts(O("ls1"), O("ls0"), -1.0, O("h8"), MUL, ADD)
             ts(O("ls2"), O("ls1"), 7, None, AND)
             copy(O("gw"), O("ls2"))
-            iota(O("wone"), [[1, 8]], 0, 0)
-            iota(O("lm"), [[1, 2], [2, 4], [0, 48]], 0, 0)
-            copy(O("xf"), O("xi"))
-            ts(O("lm"), O("lm"), O("xf"), None, EQ)
             tt(O("o1"), by(O("wone"), O("gw")), O("lm"), MUL)
             tt(O("o2"), O("o1", 0, 192), O("o1", 192, 384), ADD)
             tt(O("o3"), O("o2", 0, 96), O("o2", 96, 192), ADD)
             tt(O("o4"), O("o3", 0, 48), O("o3", 48, 96), ADD)
             copy(O("ol40"), O("o4", 0, 40))
-            spread("do1", "ow", "ol40", "y")
         tt(O("BG"), by(O("P", 0, 320), O("al%d" % t)), O("msk", 0, 320), ADD)
         scan(O("BS"), O("r16", 0, 320), O("BG"))
         ts(O("bl%d" % t), O("BS", 15, 320, 16), 160.0, None, ADD)
         spread("par%d" % t, "pl%d" % t, "ll%d" % t, "ys")
+        if t == 2:
+            spread("do1", "ow", "ol40", "y")
         for lo, hi in CH:
             off = O("pl%d" % t, lo // 16, hi // 16)
             for b in range(4):
@@ -432,17 +439,17 @@ def rank_program(g, core, T, topo):
             scores(t + 1, 1)
         else:
             copy(O("olf"), by(O("wone"), O("ow")))
-            quant("vq", "vqs", "vt", 0, 128)
-    outs = [("y", T.ol[:], T.olf[0:128:16, 0:320], [], O("olf")[1])]
+    outs = []
     for lo, hi in CH:
         o = O("qc3", lo, hi)
         outs.append(("y", T.oc[:, 4 * lo:4 * hi], codes(o)[0], [], o[1]))
     for k in range(4):
         outs.append(("y", T.osc[4 * k:4 * k + 4, 0:320], T.qs3[32 * k:32 * k + 4, 0:320], [], O("qs3")[1]))
+    outs.append(("y", T.ol[:], T.olf[0:128:16, 0:320], [], O("olf")[1]))
     for lo, hi in CH:
         p = mx("vq", 0, "qc3", lo, hi, "qs3")
         o = O("yb", lo, hi)
-        copy(o, p, "s" if lo else "v")
+        copy(o, p, "s")
         outs.append(("s", T.y[:, lo:hi], o[0], [], o[1]))
     dmas("dout", outs)
     for s in SEMAPHORES:

@@ -1,6 +1,7 @@
 from concourse.mybir import dt, AluOpType, ActivationFunctionType
 
-COPY = ActivationFunctionType.Copy
+FN = ActivationFunctionType
+COPY = FN.Copy
 ADD, SUB, MUL, MAX, MIN = AluOpType.add, AluOpType.subtract, AluOpType.mult, AluOpType.max, AluOpType.min
 BIG = 1048576.0
 C = 320
@@ -29,16 +30,17 @@ _share("iv", "int32", ("pint", 1), ("lanei", 1), ("hi", 1), ("xi", 1), ("sxi", 1
 _share("iw", "int32", ("ogr", 20), ("og7", 20), ("ls0", 24), ("ls1", 24), ("ls2", 24))
 _share("fv", "float32", ("lanef", 1), ("hf", 1), ("h8", 1), ("h2", 1), ("ux", 1), ("xf", 1), ("lan16", 1), ("lanem", 1), ("ge20", 24), ("ge40", 24), ("ja", 48), ("jf", 48))
 _share("uv", "uint16", ("pgu", 20), ("ogu", 20), ("upu", 16), ("cl", 24), ("gw", 24))
+_share("wv", "float32", *[(n, 48) for n in ("x0", "y0", "y1", "X1", "Y1", "DX", "DY", "MA", "MB", "sa0", "sb0", "sa1", "sb1", "sa2", "sb2")])
 _d("pgi", 20, "int32")
 _d("ogi", 20, "int32")
 for _n, _c in (("i16", 384), ("i8", 320), ("w320", 8), ("wone", 8),
-               ("msk", 384), ("r16", 384), ("r8", 320), ("lab", 320),
+               ("un", 384), ("ka", 384), ("msk", 384), ("r16", 384), ("r8", 320), ("lab", 320),
                ("N", 384), ("K", 384), ("DN", 192), ("KA", 192), ("KB", 192), ("KC", 192), ("MN", 192), ("E", 192), ("CC", 192),
-               ("G", 48), ("SC", 48), ("VV", 384), ("SV", 320), ("VF", 384), ("SF", 384), ("ST", 2560), ("BG", 320), ("BS", 320),
+               ("G", 48), ("SC", 48), ("G2", 48), ("SC2", 48), ("VV", 384), ("SV", 320), ("VF", 384), ("SF", 384), ("ST", 2560), ("BG", 320), ("BS", 320),
                ("rb0", 320), ("rb1", 320), ("rb2", 320), ("rb3", 320), ("lm", 384), ("o1", 384), ("o2", 192), ("o3", 96), ("o4", 48),
                ("olf", 320), ("yb", 320)):
     _d(_n, _c, "float32")
-for _n, _c in (("off", 32), ("fl0", 26), ("fl1", 26), ("fl2", 26), ("ol40", 40), ("ow", 20)):
+for _n, _c in (("off", 32), ("of2", 8), ("fl0", 26), ("fl1", 26), ("fl2", 26), ("ol40", 40), ("ow", 20)):
     _d(_n, _c, "uint16")
 for _t in range(3):
     _d("ml%d" % _t, 40, "uint16")
@@ -175,6 +177,10 @@ def rank_program(g, core, T, topo):
         else:
             run("v", [out], ins, lambda: g.vector.tensor_scalar(out[0], a[0], v1, v2, op0, op1))
 
+    def act(out, in_, func, scale, bias):
+        col = isinstance(bias, tuple)
+        run("s", [out], [in_] + [bias] * col, lambda: g.scalar.activation(out[0], in_[0], func, bias=bias[0] if col else bias, scale=scale))
+
     def scan(out, reset, data):
         run("v", [out], [reset, data], lambda: g.vector.tensor_tensor_scan(out[0], reset[0], data[0], -2.0 * BIG, MIN, MAX))
 
@@ -237,7 +243,6 @@ def rank_program(g, core, T, topo):
     copy(O("hf"), O("hi"))
     ts(O("h8"), O("hf"), 8.0, None, ADD)
     ts(O("lan16"), O("lanef"), 16.0, None, MUL)
-    ts(O("lanem"), O("lanef"), -2.0 * BIG, None, ADD)
     ts(O("pi1"), O("mi"), O("lanef"), None, ADD)
     ts(O("ge20"), O("pi1"), 20.0, -319.0, GE, MUL)
     ts(O("ge40"), O("pi1"), 40.0, -321.0, GE, MUL)
@@ -245,6 +250,13 @@ def rank_program(g, core, T, topo):
     ts(O("pi2"), O("pi0"), O("lan16"), None, ADD)
     tt(O("pi2"), O("pi2"), O("ge20"), ADD)
     copy(O("cl"), O("pi2"))
+    ts(O("h2"), O("hf"), 2.0, -160.0, MUL, ADD)
+    ts(O("jf"), O("ja"), O("h2"), None, ADD)
+    tt(O("sxi"), O("hi"), O("xi"), SUB)
+    ts(O("sx7"), O("sxi"), 7, None, AND)
+    ts(O("ux"), O("sx7"), -320.0, -160.0, MUL, ADD)
+    ts(O("lanem"), O("lanef"), -BIG, 2.0 * BIG * BIG, MUL, ADD)
+    act(O("msk"), O("i16"), FN.Abs, BIG, O("lanem"))
     copy(O("pgu"), O("pgi"))
     copy(O("P", 0, 320), by(O("i320"), O("pgu")))
     items = []
@@ -261,18 +273,11 @@ def rank_program(g, core, T, topo):
     ts(O("ogr"), O("ogi"), -1.0, O("h8"), MUL, ADD)
     ts(O("og7"), O("ogr"), 7, None, AND)
     copy(O("ogu"), O("og7"))
-    copy(O("lab"), by(O("w320"), O("ogu")))
-    ts(O("h2"), O("hf"), 2.0, -160.0, MUL, ADD)
-    ts(O("jf"), O("ja"), O("h2"), None, ADD)
-    ts(O("msk"), O("i16"), O("lanem"), -BIG, NE, MUL)
-    tt(O("N"), by(O("lab"), O("cl")), O("msk"), ADD)
-
-    copy(O("upu"), O("upi"))
-    quant("uq", "uqs", "ut", 0, 128)
-    copy(words(O("uw")), by(words(O("uq")), O("upu")))
-    copy(O("uws"), by(O("uqs"), O("upu")), "s")
-    for lo, hi in CH:
-        quant("qc0", "qs0", "xt0", lo, hi)
+    copy(O("lab"), by(O("w320"), O("ogu")), "s")
+    tt(O("N"), by(O("lab"), O("cl")), O("msk"), SUB)
+    copy(O("un"), by(O("lab"), O("cl")), "s")
+    act(O("ka"), O("un"), FN.Abs, 1.0, O("ux"))
+    act(O("K"), O("ka"), FN.Relu, -1.0, 1.0)
 
     def scores(t, piece):
         lo, hi = CH[piece]
@@ -285,7 +290,7 @@ def rank_program(g, core, T, topo):
 
     def send(t, out, in_, sem):
         rid, pid, _s = topo.addr(partner[t])
-        eng = topo.engines(core, partner[t])[::2]
+        eng = topo.engines(core, partner[t])
         order("g", in_[1], [])
         g.remote_dma(out[0], in_[0], T.sem[sem], T.sem.left, pid=pid, routing_id=rid, dma_engine_mask=sum(1 << e for e in eng))
         total["left"] += len(eng)
@@ -296,28 +301,47 @@ def rank_program(g, core, T, topo):
         n += send(t, O("lp%d" % t), O("qs%d" % t), "rq%d" % t)
         arrives("rq%d" % t, n, [O("lc%d" % t), O("lp%d" % t)])
 
-    send_state(0)
-    scores(0, 0)
-    scores(0, 1)
-
-    def P_by(k):
-        return by(O("P"), O("off", 4 * k, 4 * k + 3))
+    def P_by(k, name="off"):
+        return by(O("P"), O(name, 4 * k, 4 * k + 3))
 
     def place(name, k):
         return O(name, 48 * slot(k), 48 * slot(k) + 48)
 
-    def walk(beside):
-        tt(O("G"), place("N", 0), O("jf"), ADD)
-        for k in range(8):
+    def walk(start, k0, beside):
+        tt(O("G"), start, place("N", k0), ADD)
+        for call in beside[0]:
+            call()
+        for k in range(k0, 8):
             scan(O("SC"), O("r16", 0, 48), O("G"))
             copy(O("off", 4 * k, 4 * k + 3), O("SC", 15, 48, 16))
             if k < 7:
                 tt(O("G"), P_by(k), place("N", k + 1), ADD)
-            for call in beside[k]:
+            for call in beside[k - k0 + 1]:
                 call()
 
-    def score_places(k):
-        tt(place("VF", k), P_by(k), place("N", k), ADD)
+    first = [0, 1, 0]
+    FROM, NX, NY = ["jf", "sa0", "jf"], ["x0", "sb0", "sa0"], ["y0", "y1", "sa1"]
+
+    def ahead(t):
+        f = first[t]
+        return [lambda: tt(O("G2"), O(FROM[t]), place("N", f + 1), ADD),
+                lambda: scan(O("SC2"), O("r16", 0, 48), O("G2")),
+                lambda: copy(O("of2", 0, 3), O("SC2", 15, 48, 16)),
+                lambda: tt(O("G2"), P_by(0, "of2"), place("N", f), ADD),
+                lambda: copy(O("X1"), P_by(0, "of2"), "s"),
+                lambda: scan(O("SC2"), O("r16", 0, 48), O("G2")),
+                lambda: tt(O("DX"), O("X1"), O(NX[t]), SUB),
+                lambda: copy(O("of2", 4, 7), O("SC2", 15, 48, 16)),
+                lambda: copy(O("Y1"), P_by(1, "of2"), "s"),
+                lambda: tt(O("DY"), O("Y1"), O(NY[t]), SUB)]
+
+    def address(t, k):
+        if k in (first[t], first[t] + 1):
+            return O(("sa%d" if k == first[t] else "sb%d") % t)
+        return O("sa0") if k < first[t] else P_by(k)
+
+    def score_places(t, k):
+        tt(place("VF", k), P_by(k) if t < 0 else address(t, k), place("N", k), ADD)
 
     def score_list(t):
         scan(O("SF"), O("r16"), O("VF"))
@@ -327,18 +351,6 @@ def rank_program(g, core, T, topo):
         else:
             copy(O("fl%d" % t, 0, 24), O("SF", 15, 384, 16))
 
-    walk([[lambda k=k: score_places(k)] for k in range(8)])
-    score_list(0)
-    quant("eq", "eqs", "ec", 0, 512)
-    iota(O("i8"), [[0, 40], [1, 8]], 0, 0)
-    select(O("r8"), O("i8"), [[0, 40], [1, 8]], 1.0)
-    iota(O("wone"), [[1, 8]], 0, 0)
-    iota(O("lm"), [[1, 2], [2, 4], [0, 48]], 0, 0)
-
-    tt(O("sxi"), O("hi"), O("xi"), SUB)
-    ts(O("sx7"), O("sxi"), 7, None, AND)
-    ts(O("ux"), O("sx7"), 320.0, 160.0, MUL, ADD)
-    ts(O("K"), by(O("lab"), O("cl")), O("ux"), None, EQ)
 
     def sides(t):
         return ((192, 336), (48, 192)) if t == 1 else ((0, 192), (192, 384))
@@ -346,10 +358,10 @@ def rank_program(g, core, T, topo):
     def differences(t):
         a, b = sides(t)
         n = a[1] - a[0]
-        tt(O("DN", 0, n), O("N", *b), O("N", *a), SUB)
-        ts(O("KC", 0, n), O("K", *b), 2.0, -1.0, MUL, ADD)
-        tt(O("KA", 0, n), O("KC", 0, n), O("K", *a), ADD)
-        ts(O("KB", 0, n), O("KA", 0, n), -1.0, 1.0, MUL, ADD)
+        return [lambda: tt(O("DN", 0, n), O("N", *b), O("N", *a), SUB),
+                lambda: act(O("KC", 0, n), O("K", *b), FN.Identity, 2.0, -1.0),
+                lambda: tt(O("KA", 0, n), O("KC", 0, n), O("K", *a), ADD),
+                lambda: act(O("KB", 0, n), O("KA", 0, n), FN.Identity, -1.0, 1.0)]
 
     def exchange(t):
         a, b = sides(t)
@@ -360,8 +372,14 @@ def rank_program(g, core, T, topo):
                 lambda: tt(O("K", *a), O("KA", 0, n), O("CC", 0, n), EQ),
                 lambda: tt(O("K", *b), O("KB", 0, n), O("CC", 0, n), EQ)]
 
-    def pick(k):
-        tt(O("VV", k, 384, 8), P_by(k), place("K", k), MUL)
+    def choose(t):
+        return [lambda: tt(O("MB"), O("DY"), O("CC", 0, 48), MUL),
+                lambda: tt(O("sb%d" % t), O(NY[t]), O("MB"), ADD),
+                lambda: tt(O("MA"), O("DX"), O("CC", 0, 48), MUL),
+                lambda: tt(O("sa%d" % t), O(NX[t]), O("MA"), ADD)]
+
+    def pick(t, k):
+        tt(O("VV", k, 384, 8), address(t, k), place("K", k), MUL)
 
     def spread(sem, out, in_, qs):
         dmas(sem, [(qs[i % len(qs)], T[out][16 * i:16 * i + 16, 0:20], T[in_][i:128:16, 0:40], [(out, 0, 20, 1, 0)], [(in_, 0, 40, 1, 0)])
@@ -372,19 +390,42 @@ def rank_program(g, core, T, topo):
             p = mx("eq", 128 * b, cn, 0, 320, sn)
             copy(O("%s%d" % (name, t), 320 * b, 320 * b + 320), p, "s")
 
-    differences(0)
+    sp, df, vf = ahead(0), differences(0), [lambda k=k: score_places(-1, k) for k in range(8)]
+    walk(O("jf"), 0, [
+        [lambda: copy(O("upu"), O("upi")), lambda: quant("uq", "uqs", "ut", 0, 128)],
+        [lambda: copy(words(O("uw")), by(words(O("uq")), O("upu"))), sp[0]],
+        [lambda: quant("qc0", "qs0", "xt0", *CH[0]), lambda: quant("qc0", "qs0", "xt0", *CH[1]), sp[1],
+         lambda: copy(O("uws"), by(O("uqs"), O("upu")), "s"), lambda: scores(0, 0)],
+        [lambda: copy(O("x0"), P_by(0), "s"), lambda: copy(O("y0"), P_by(1), "s"), df[1], sp[2], df[0]],
+        [sp[3], sp[4], lambda: scores(0, 1), vf[0], vf[1]],
+        [sp[5], vf[2], vf[3], sp[6]],
+        [sp[7], df[2], vf[4]],
+        [df[3], sp[8], vf[5]],
+        [vf[6], vf[7]]])
+    score_list(0)
+    sp[9]()
+    send_state(0)
+    quant("eq", "eqs", "ec", 0, 512)
+    iota(O("i8"), [[0, 40], [1, 8]], 0, 0)
+    select(O("r8"), O("i8"), [[0, 40], [1, 8]], 1.0)
+    iota(O("wone"), [[1, 8]], 0, 0)
+    iota(O("lm"), [[1, 2], [2, 4], [0, 48]], 0, 0)
+
     for t in range(3):
         n = sides(t)[0][1] - sides(t)[0][0]
         unpack(t, "fo", "qc%d" % t, "qs%d" % t)
         unpack(t, "fp", "lc%d" % t, "lp%d" % t)
-        first, second = ((14, 23), (4, 13)) if t == 1 else ((0, 12), (12, 24))
-        copy(O("E", 0, n), by(O("ST"), O("fl%d" % t, *first)))
-        tt(O("CC", 0, n), by(O("ST"), O("fl%d" % t, *second)), O("E", 0, n), LT)
-        ex = exchange(t)
-        for call in ex[:3]:
+        one, two = ((14, 23), (4, 13)) if t == 1 else ((0, 12), (12, 24))
+        copy(O("E", 0, n), by(O("ST"), O("fl%d" % t, *one)))
+        tt(O("CC", 0, n), by(O("ST"), O("fl%d" % t, *two)), O("E", 0, n), LT)
+        ex, ch = exchange(t), choose(t)
+        for call in (ex[0], ch[0], ex[1], ch[1]):
             call()
-        p = [lambda k=k: pick(k) for k in range(8)]
-        walk([ex[3:4], ex[4:5], p[0:2], p[2:3], p[3:4], p[4:6], p[6:7], p[7:]])
+        p = [lambda k=k: pick(t, k) for k in range(8)]
+        if t == 1:
+            walk(O("sb1"), 3, [ex[2:3], ex[3:4], ex[4:5] + ch[2:3], ch[3:4] + p[3:5], [p[0], p[1], p[2], p[5], p[6]], p[7:]])
+        else:
+            walk(O("sb%d" % t), 2, [ex[2:3], ex[3:4], ex[4:5] + ch[2:3], ch[3:4] + p[2:4], [p[0], p[1], p[4]], p[5:7], p[7:]])
         run("v", [O("SV")], [O("r8"), O("VV", 0, 320)],
             lambda: g.vector.tensor_tensor_scan(O("SV")[0], O("r8")[0], O("VV", 0, 320)[0], 0.0, MUL, ADD))
         ts(O("ml%d" % t), O("SV", 7, 320, 8), 160.0, None, ADD)
@@ -392,14 +433,14 @@ def rank_program(g, core, T, topo):
         arrives("rl%d" % t, k, [O("ll%d" % t)])
         spread("own%d" % t, "al%d" % t, "ml%d" % t, "y")
         if t < 2:
-            for k in range(8):
-                score_places(k)
-            score_list(t + 1)
-            differences(t + 1)
             if t == 0:
-                quant("vq", "vqs", "vt", 0, 128)
-                copy(O("xf"), O("xi"))
-                ts(O("lm"), O("lm"), O("xf"), None, EQ)
+                copy(O("y1"), P_by(2), "s")
+            sp, df, vf = ahead(t + 1), differences(t + 1), [lambda k=k: score_places(t, k) for k in range(8)]
+            for call in (df[1:2] + sp[0:1] + vf[0:2] + sp[1:2] + vf[2:4] + sp[2:3] + df[2:3] + sp[3:5] + df[3:4] + vf[4:5] + sp[5:6] + vf[5:7]
+                         + sp[7:9] + vf[7:8] + sp[6:7] + df[0:1]):
+                call()
+            score_list(t + 1)
+            sp[9]()
         else:
             scan(O("SF"), O("r16"), O("N"))
             ts(O("ls0"), O("SF", 15, 384, 16), -160.0, 1.0 / 320.0, ADD, MUL)
@@ -411,7 +452,7 @@ def rank_program(g, core, T, topo):
             tt(O("o3"), O("o2", 0, 96), O("o2", 96, 192), ADD)
             tt(O("o4"), O("o3", 0, 48), O("o3", 48, 96), ADD)
             copy(O("ol40"), O("o4", 0, 40))
-        tt(O("BG"), by(O("P", 0, 320), O("al%d" % t)), O("msk", 0, 320), ADD)
+        tt(O("BG"), by(O("P", 0, 320), O("al%d" % t)), O("msk", 0, 320), SUB)
         scan(O("BS"), O("r16", 0, 320), O("BG"))
         ts(O("bl%d" % t), O("BS", 15, 320, 16), 160.0, None, ADD)
         spread("par%d" % t, "pl%d" % t, "ll%d" % t, "ys")
@@ -422,6 +463,10 @@ def rank_program(g, core, T, topo):
             for b in range(4):
                 copy(O("zt%d" % t, 4 * lo + b, 4 * hi, 4), by(O("fp%d" % t, 320 * b, 320 * b + 320), off), "v" if b < 2 else "s")
             quant("zc%d" % t, "zs%d" % t, "zt%d" % t, lo, hi)
+        if t == 0:
+            quant("vq", "vqs", "vt", 0, 128)
+            copy(O("xf"), O("xi"))
+            ts(O("lm"), O("lm"), O("xf"), None, EQ)
         for lo, hi in CH:
             for b in range(4):
                 p = mx("wq", 128 * b, "zc%d" % t, lo, hi, "zs%d" % t)

from concourse.mybir import dt, AluOpType, ActivationFunctionType

FN = ActivationFunctionType
COPY = FN.Copy
ADD, SUB, MUL, MAX, MIN = AluOpType.add, AluOpType.subtract, AluOpType.mult, AluOpType.max, AluOpType.min
BIG = 1048576.0
C = 320
STEP = [1, 2, 4]
CH = [(0, 192), (192, 320)]

SCRATCH = {}


def _d(name, cols, dtype, where="sbuf"):
    SCRATCH[name] = (where, [128, cols], dtype)


ALIAS = {}


def _share(buf, dtype, *parts):
    at = 0
    for n, c in parts:
        ALIAS[n] = (buf, at, c)
        at += c + c % 2
    _d(buf, at, dtype)


_share("iv", "int32", ("pint", 1), ("lanei", 1), ("hi", 1), ("xi", 1), ("sxi", 1), ("sx7", 1), ("upi", 16), ("mi", 24), ("pi0", 24), ("pi1", 24), ("pi2", 24))
_share("iw", "int32", ("ogr", 20), ("og7", 20), ("ls0", 24), ("ls1", 24), ("ls2", 24))
_share("fv", "float32", ("lanef", 1), ("hf", 1), ("h8", 1), ("h2", 1), ("ux", 1), ("xf", 1), ("lan16", 1), ("lanem", 1), ("ge20", 24), ("ge40", 24), ("ja", 48), ("jf", 48))
_share("uv", "uint16", ("pgu", 20), ("ogu", 20), ("upu", 16), ("cl", 24), ("gw", 24))
_share("wv", "float32", *[(n, 48) for n in ("x0", "y0", "y1", "X1", "Y1", "DX", "DY", "MA", "MB", "sa0", "sb0", "sa1", "sb1", "sa2", "sb2")])
_d("pgi", 20, "int32")
_d("ogi", 20, "int32")
for _n, _c in (("i16", 384), ("i8", 320), ("w320", 8), ("wone", 8),
               ("un", 384), ("ka", 384), ("msk", 384), ("r16", 384), ("r8", 320), ("lab", 320),
               ("N", 384), ("K", 384), ("DN", 192), ("KA", 192), ("KB", 192), ("KC", 192), ("MN", 192), ("E", 192), ("CC", 192),
               ("G", 48), ("SC", 48), ("G2", 48), ("SC2", 48), ("VV", 384), ("SV", 320), ("VF", 384), ("SF", 384), ("ST", 2560), ("BG", 320), ("BS", 320),
               ("rb0", 320), ("rb1", 320), ("rb2", 320), ("rb3", 320), ("lm", 384), ("o1", 384), ("o2", 192), ("o3", 96), ("o4", 48),
               ("olf", 320), ("yb", 320)):
    _d(_n, _c, "float32")
for _n, _c in (("off", 32), ("of2", 8), ("fl0", 26), ("fl1", 26), ("fl2", 26), ("ol40", 40), ("ow", 20)):
    _d(_n, _c, "uint16")
for _t in range(3):
    _d("ml%d" % _t, 40, "uint16")
    _d("ll%d" % _t, 40, "uint16")
    _d("al%d" % _t, 20, "uint16")
    _d("pl%d" % _t, 20, "uint16")
    _d("bl%d" % _t, 20, "uint16")
    _d("fo%d" % _t, 1280, "bfloat16")
    _d("fp%d" % _t, 1280, "bfloat16")
    _d("zt%d" % _t, 1280, "bfloat16")
    _d("zc%d" % _t, 320, "float8_e4m3fn_x4")
    _d("zs%d" % _t, 320, "uint8")
    _d("lc%d" % _t, 320, "float8_e4m3fn_x4")
    _d("lp%d" % _t, 320, "uint8")
for _t in range(4):
    _d("xt%d" % _t, 1280, "bfloat16")
    _d("qc%d" % _t, 320, "float8_e4m3fn_x4")
    _d("qs%d" % _t, 320, "uint8")
for _n, _c in (("i320", 320), ("P", 2560), ("ones", 512), ("ec", 2048), ("ut", 512), ("vt", 512)):
    _d(_n, _c, "bfloat16")
for _n, _c in (("eq", 512), ("wq", 512), ("uq", 128), ("uw", 256), ("vq", 128)):
    _d(_n, _c, "float8_e4m3fn_x4")
    _d(_n + "s", _c, "uint8")
for _k in range(8):
    _d("ps%d" % _k, 512, "float32", "psum")

DMA_SEMS = ["dpg", "dog", "du", "dxa", "dxb", "dw", "dv", "dp", "own0", "own1", "own2", "par0", "par1", "par2", "do1", "do2", "dout"]
SEMAPHORES = ["cv", "cs", "ct", "cg", "left", "rq0", "rq1", "rq2", "rl0", "rl1", "rl2"] + DMA_SEMS


def slot(k):
    return k // 2 + (4 if k % 2 else 0)


def rank_program(g, core, T, topo):
    rank = T.rank_of(core)
    if rank is None:
        return
    queue = {"v": g.vector, "s": g.scalar, "t": g.tensor, "g": g, "y": g.sync}
    total = {s: 0 for s in SEMAPHORES}
    clock = {q: {} for q in queue}
    wrote, read = {}, {}

    def O(name, lo=0, hi=None, step=1):
        if name in ALIAS:
            name, at, n = ALIAS[name]
            lo, hi = at + lo, at + (n if hi is None else hi)
        hi = SCRATCH[name][1][1] if hi is None else hi
        ap = T[name][:, lo:hi] if step == 1 else T[name][:, lo:hi:step]
        return (ap, [(name, lo, hi, step, lo % step)])

    def codes(o):
        return (o[0].bitcast(dt.uint8), o[1])

    def words(o):
        return (o[0].bitcast(dt.uint32), o[1])

    def by(win, off):
        return (win[0].indirect(off[0]), win[1] + off[1])

    def meet(a, b):
        return a[1] < b[2] and b[1] < a[2] and not (a[3] == b[3] > 1 and a[4] != b[4])

    def order(q, reads, writes, dma=False):
        evs = []
        writes = writes + [r for r in reads if r[0][:2] == "ps"]
        for r in reads:
            evs += [e for w, e in wrote.get(r[0], []) if meet(r, w)]
        for r in writes:
            evs += [e for w, e in wrote.get(r[0], []) if meet(r, w)]
            evs += [e for w, e in read.get(r[0], []) if meet(r, w) and (dma or e[3] != q)]
        want = {}
        for sem, val, snap, who in evs:
            if clock[q].get(sem, 0) < val and want.get(sem, (0,))[0] < val:
                want[sem] = (val, snap)
        for sem in list(want):
            if any(o != sem and want[o][1].get(sem, 0) >= want[sem][0] for o in want):
                del want[sem]
        for sem, (val, snap) in want.items():
            queue[q].wait_ge(T.sem[sem], val)
            for s2, v2 in list(snap.items()) + [(sem, val)]:
                clock[q][s2] = max(clock[q].get(s2, 0), v2)

    def note(reads, writes, ev):
        for r in reads:
            read.setdefault(r[0], []).append((r, ev))
        for w in writes:
            old = wrote.get(w[0], [])
            wrote[w[0]] = [(o, e) for o, e in old if not (w[3] == 1 and w[1] <= o[1] and o[2] <= w[2])] + [(w, ev)]
            if w[0] in read:
                read[w[0]] = [(o, e) for o, e in read[w[0]] if not (w[3] == 1 and w[1] <= o[1] and o[2] <= w[2])]

    def run(q, outs, ins, call):
        reads = [r for o in ins for r in o[1]]
        writes = [r for o in outs for r in o[1]]
        order(q, reads, writes)
        sem = "c" + q
        total[sem] += 1
        snap = dict(clock[q])
        call().then_inc(T.sem[sem], 1)
        note(reads, writes, (sem, total[sem], snap, q))

    def dmas(sem, items):
        snap, acc = {}, []
        for q, out, in_, writes, reads in items:
            order(q, reads, writes, True)
            queue[q].dma_start(out, in_).then_inc(T.sem[sem], 16)
            total[sem] += 16
            for s2, v2 in clock[q].items():
                snap[s2] = max(snap.get(s2, 0), v2)
            acc.append((reads, writes))
        for reads, writes in acc:
            note(reads, writes, (sem, total[sem], snap, "dma"))

    def arrives(sem, val, outs):
        total[sem] += val
        note([], [r for o in outs for r in o[1]], (sem, val, {}, "far"))

    def copy(out, in_, q="v"):
        if q == "v":
            run(q, [out], [in_], lambda: g.vector.tensor_copy(out[0], in_[0]))
        else:
            run(q, [out], [in_], lambda: g.scalar.activation(out[0], in_[0], COPY))

    def tt(out, a, b, op):
        run("v", [out], [a, b], lambda: g.vector.tensor_tensor(out[0], a[0], b[0], op))

    def ts(out, a, s1, s2, op0, op1=None):
        ins = [a] + [s for s in (s1, s2) if isinstance(s, tuple)]
        v1 = s1[0] if isinstance(s1, tuple) else s1
        v2 = s2[0] if isinstance(s2, tuple) else s2
        if op1 is None:
            run("v", [out], ins, lambda: g.vector.tensor_scalar(out[0], a[0], v1, None, op0))
        else:
            run("v", [out], ins, lambda: g.vector.tensor_scalar(out[0], a[0], v1, v2, op0, op1))

    def act(out, in_, func, scale, bias):
        col = isinstance(bias, tuple)
        run("s", [out], [in_] + [bias] * col, lambda: g.scalar.activation(out[0], in_[0], func, bias=bias[0] if col else bias, scale=scale))

    def scan(out, reset, data):
        run("v", [out], [reset, data], lambda: g.vector.tensor_tensor_scan(out[0], reset[0], data[0], -2.0 * BIG, MIN, MAX))

    def iota(out, pattern, base, mul):
        kw = {} if SCRATCH[out[1][0][0]][2] == "int32" else {"allow_small_or_imprecise_dtypes": True}
        run("g", [out], [], lambda: g.iota(out[0], pattern, base, mul, **kw))

    def quant(cn, sn, xn, lo, hi):
        q, s, x = O(cn, lo, hi), O(sn, lo, hi), O(xn, 4 * lo, 4 * hi)
        run("v", [q, s], [x], lambda: g.vector.quantize_mx(q[0], s[0], x[0]))

    bank = [0]

    def mx(an, alo, bn, lo, hi, bsn=None, asn=None):
        k = bank[0] % 8
        bank[0] += 1
        out = O("ps%d" % k, 0, hi - lo)
        full = (out[0], [("ps%d" % k, 0, 512, 1, 0)])
        a, s = O(an, alo, alo + 128), O(asn or an + "s", alo, alo + 128)
        b, p = O(bn, lo, hi), O(bsn, lo, hi)
        run("t", [full], [a, s, b, p], lambda: g.tensor.matmul_mx(out[0], a[0], s[0], b[0], p[0], True, True))
        return full

    def load(q, name, src, lo, hi, fn=None):
        o = O(name, lo, hi)
        return (q, (fn(o) if fn else o)[0], src, o[1], [])

    dmas("dpg", [load("y", "pgi", T.pg[:], 0, 20)])
    dmas("dog", [("s" if d else "y", T.ogi[2 * k + d:128:16, 0:20], T.og[16 * k + d:16 * k + 16:2, 0:20], [("ogi", 0, 20, 1, 0)], [])
                 for k in range(8) for d in range(2)])
    dmas("du", [load("s", "ut", T.u[:], 0, 512)])
    dmas("dxa", [load("y", "xt0", T.x[:, 0:768], 0, 768)])
    dmas("dxb", [load("y", "xt0", T.x[:, 768:1280], 768, 1280)])

    AND, SHR, EQ, NE, GE, LT = (AluOpType.bitwise_and, AluOpType.arith_shift_right, AluOpType.is_equal, AluOpType.not_equal,
                                AluOpType.is_ge, AluOpType.is_lt)

    def select(out, in_, pattern, fill, base=0, mul=0):
        run("g", [out], [in_], lambda: g.affine_select(out[0], in_[0], pattern, EQ, fill, base, mul))

    iota(O("pint"), [[1, 1]], 0, 1)
    iota(O("mi"), [[0, 8], [16, 3]], 0, 0)
    iota(O("pi0"), [[2, 2], [4, 4], [256, 3]], 0, 0)
    iota(O("i320"), [[1, 320]], -160, 0)
    iota(O("ja", 0, 40), [[1, 2], [16, 20]], 0, 0)
    iota(O("ja", 40, 48), [[16, 8]], 0, 0)
    iota(O("w320"), [[320, 8]], 160, 0)
    iota(O("upi"), [[0, 2], [16, 8]], 0, 0)
    iota(O("i16"), [[0, 24], [1, 16]], -2097152, 0)
    select(O("r16"), O("i16"), [[0, 24], [1, 16]], 2.0 * BIG)
    for b in range(4):
        if b == 0:
            run("v", [O("ones")], [], lambda: g.vector.memset(O("ones")[0], 1.0))
        select(O("ec", 512 * b, 512 * b + 512), O("ones"), [[-1, 512]], 0.0, b, 4)

    ts(O("lanei"), O("pint"), 15, None, AND)
    ts(O("hi"), O("pint"), 4, None, SHR)
    ts(O("xi"), O("pint"), 7, None, AND)
    copy(O("lanef"), O("lanei"))
    copy(O("hf"), O("hi"))
    ts(O("h8"), O("hf"), 8.0, None, ADD)
    ts(O("lan16"), O("lanef"), 16.0, None, MUL)
    ts(O("pi1"), O("mi"), O("lanef"), None, ADD)
    ts(O("ge20"), O("pi1"), 20.0, -319.0, GE, MUL)
    ts(O("ge40"), O("pi1"), 40.0, -321.0, GE, MUL)
    tt(O("ge20"), O("ge20"), O("ge40"), ADD)
    ts(O("pi2"), O("pi0"), O("lan16"), None, ADD)
    tt(O("pi2"), O("pi2"), O("ge20"), ADD)
    copy(O("cl"), O("pi2"))
    ts(O("h2"), O("hf"), 2.0, -160.0, MUL, ADD)
    ts(O("jf"), O("ja"), O("h2"), None, ADD)
    tt(O("sxi"), O("hi"), O("xi"), SUB)
    ts(O("sx7"), O("sxi"), 7, None, AND)
    ts(O("ux"), O("sx7"), -320.0, -160.0, MUL, ADD)
    ts(O("lanem"), O("lanef"), -BIG, 2.0 * BIG * BIG, MUL, ADD)
    act(O("msk"), O("i16"), FN.Abs, BIG, O("lanem"))
    copy(O("pgu"), O("pgi"))
    copy(O("P", 0, 320), by(O("i320"), O("pgu")))
    items = []
    for s in range(1, 8):
        w = [("P", 320 * s, 320 * s + 320, 1, 0)]
        r = [("P", 0, 320, 1, 0)]
        q = "y" if s % 2 else "s"
        items.append((q, T.P[16 * s:128, 320 * s:320 * s + 320], T.P[0:128 - 16 * s, 0:320], w, r))
        items.append((q, T.P[0:16 * s, 320 * s:320 * s + 320], T.P[128 - 16 * s:128, 0:320], w, r))
    dmas("dp", items)
    dmas("dw", [("y", codes(O("wq"))[0], T.wc[:], O("wq")[1], []), ("y", O("wqs")[0], T.ws[:], O("wqs")[1], [])])
    dmas("dv", [load("y", "vt", T.v[:], 0, 512)])

    ts(O("ogr"), O("ogi"), -1.0, O("h8"), MUL, ADD)
    ts(O("og7"), O("ogr"), 7, None, AND)
    copy(O("ogu"), O("og7"))
    copy(O("lab"), by(O("w320"), O("ogu")), "s")
    tt(O("N"), by(O("lab"), O("cl")), O("msk"), SUB)
    copy(O("un"), by(O("lab"), O("cl")), "s")
    act(O("ka"), O("un"), FN.Abs, 1.0, O("ux"))
    act(O("K"), O("ka"), FN.Relu, -1.0, 1.0)

    def scores(t, piece):
        lo, hi = CH[piece]
        for s in range(8):
            p = mx("uw", 16 * (8 - s), "qc%d" % t, lo, hi, "qs%d" % t)
            q = "v" if t and piece and s % 2 else "s"
            copy(O("ST", 320 * s + lo, 320 * s + hi), (p[0], p[1]), q)

    partner = [T.cores[rank ^ s] for s in STEP]

    def send(t, out, in_, sem):
        rid, pid, _s = topo.addr(partner[t])
        eng = topo.engines(core, partner[t])
        order("g", in_[1], [])
        g.remote_dma(out[0], in_[0], T.sem[sem], T.sem.left, pid=pid, routing_id=rid, dma_engine_mask=sum(1 << e for e in eng))
        total["left"] += len(eng)
        return len(eng)

    def send_state(t):
        n = send(t, codes(O("lc%d" % t)), codes(O("qc%d" % t)), "rq%d" % t)
        n += send(t, O("lp%d" % t), O("qs%d" % t), "rq%d" % t)
        arrives("rq%d" % t, n, [O("lc%d" % t), O("lp%d" % t)])

    def P_by(k, name="off"):
        return by(O("P"), O(name, 4 * k, 4 * k + 3))

    def place(name, k):
        return O(name, 48 * slot(k), 48 * slot(k) + 48)

    def walk(start, k0, beside):
        tt(O("G"), start, place("N", k0), ADD)
        for call in beside[0]:
            call()
        for k in range(k0, 8):
            scan(O("SC"), O("r16", 0, 48), O("G"))
            copy(O("off", 4 * k, 4 * k + 3), O("SC", 15, 48, 16))
            if k < 7:
                tt(O("G"), P_by(k), place("N", k + 1), ADD)
            for call in beside[k - k0 + 1]:
                call()

    first = [0, 1, 0]
    FROM, NX, NY = ["jf", "sa0", "jf"], ["x0", "sb0", "sa0"], ["y0", "y1", "sa1"]

    def ahead(t):
        f = first[t]
        return [lambda: tt(O("G2"), O(FROM[t]), place("N", f + 1), ADD),
                lambda: scan(O("SC2"), O("r16", 0, 48), O("G2")),
                lambda: copy(O("of2", 0, 3), O("SC2", 15, 48, 16)),
                lambda: tt(O("G2"), P_by(0, "of2"), place("N", f), ADD),
                lambda: copy(O("X1"), P_by(0, "of2"), "s"),
                lambda: scan(O("SC2"), O("r16", 0, 48), O("G2")),
                lambda: tt(O("DX"), O("X1"), O(NX[t]), SUB),
                lambda: copy(O("of2", 4, 7), O("SC2", 15, 48, 16)),
                lambda: copy(O("Y1"), P_by(1, "of2"), "s"),
                lambda: tt(O("DY"), O("Y1"), O(NY[t]), SUB)]

    def address(t, k):
        if k in (first[t], first[t] + 1):
            return O(("sa%d" if k == first[t] else "sb%d") % t)
        return O("sa0") if k < first[t] else P_by(k)

    def score_places(t, k):
        tt(place("VF", k), P_by(k) if t < 0 else address(t, k), place("N", k), ADD)

    def score_list(t):
        scan(O("SF"), O("r16"), O("VF"))
        if t == 1:
            copy(O("fl1", 1, 13), O("SF", 15, 192, 16))
            copy(O("fl1", 14, 26), O("SF", 207, 384, 16))
        else:
            copy(O("fl%d" % t, 0, 24), O("SF", 15, 384, 16))


    def sides(t):
        return ((192, 336), (48, 192)) if t == 1 else ((0, 192), (192, 384))

    def differences(t):
        a, b = sides(t)
        n = a[1] - a[0]
        return [lambda: tt(O("DN", 0, n), O("N", *b), O("N", *a), SUB),
                lambda: act(O("KC", 0, n), O("K", *b), FN.Identity, 2.0, -1.0),
                lambda: tt(O("KA", 0, n), O("KC", 0, n), O("K", *a), ADD),
                lambda: act(O("KB", 0, n), O("KA", 0, n), FN.Identity, -1.0, 1.0)]

    def exchange(t):
        a, b = sides(t)
        n = a[1] - a[0]
        return [lambda: tt(O("MN", 0, n), O("DN", 0, n), O("CC", 0, n), MUL),
                lambda: tt(O("N", *a), O("N", *a), O("MN", 0, n), ADD),
                lambda: tt(O("N", *b), O("N", *b), O("MN", 0, n), SUB),
                lambda: tt(O("K", *a), O("KA", 0, n), O("CC", 0, n), EQ),
                lambda: tt(O("K", *b), O("KB", 0, n), O("CC", 0, n), EQ)]

    def choose(t):
        return [lambda: tt(O("MB"), O("DY"), O("CC", 0, 48), MUL),
                lambda: tt(O("sb%d" % t), O(NY[t]), O("MB"), ADD),
                lambda: tt(O("MA"), O("DX"), O("CC", 0, 48), MUL),
                lambda: tt(O("sa%d" % t), O(NX[t]), O("MA"), ADD)]

    def pick(t, k):
        tt(O("VV", k, 384, 8), address(t, k), place("K", k), MUL)

    def spread(sem, out, in_, qs):
        dmas(sem, [(qs[i % len(qs)], T[out][16 * i:16 * i + 16, 0:20], T[in_][i:128:16, 0:40], [(out, 0, 20, 1, 0)], [(in_, 0, 40, 1, 0)])
                   for i in range(8)])

    def unpack(t, name, cn, sn):
        for b in range(4):
            p = mx("eq", 128 * b, cn, 0, 320, sn)
            copy(O("%s%d" % (name, t), 320 * b, 320 * b + 320), p, "s")

    sp, df, vf = ahead(0), differences(0), [lambda k=k: score_places(-1, k) for k in range(8)]
    walk(O("jf"), 0, [
        [lambda: copy(O("upu"), O("upi")), lambda: quant("uq", "uqs", "ut", 0, 128)],
        [lambda: copy(words(O("uw")), by(words(O("uq")), O("upu"))), sp[0]],
        [lambda: quant("qc0", "qs0", "xt0", *CH[0]), lambda: quant("qc0", "qs0", "xt0", *CH[1]), sp[1],
         lambda: copy(O("uws"), by(O("uqs"), O("upu")), "s"), lambda: scores(0, 0)],
        [lambda: copy(O("x0"), P_by(0), "s"), lambda: copy(O("y0"), P_by(1), "s"), df[1], sp[2], df[0]],
        [sp[3], sp[4], lambda: scores(0, 1), vf[0], vf[1]],
        [sp[5], vf[2], vf[3], sp[6]],
        [sp[7], df[2], vf[4]],
        [df[3], sp[8], vf[5]],
        [vf[6], vf[7]]])
    score_list(0)
    sp[9]()
    send_state(0)
    quant("eq", "eqs", "ec", 0, 512)
    iota(O("i8"), [[0, 40], [1, 8]], 0, 0)
    select(O("r8"), O("i8"), [[0, 40], [1, 8]], 1.0)
    iota(O("wone"), [[1, 8]], 0, 0)
    iota(O("lm"), [[1, 2], [2, 4], [0, 48]], 0, 0)

    for t in range(3):
        n = sides(t)[0][1] - sides(t)[0][0]
        unpack(t, "fo", "qc%d" % t, "qs%d" % t)
        unpack(t, "fp", "lc%d" % t, "lp%d" % t)
        one, two = ((14, 23), (4, 13)) if t == 1 else ((0, 12), (12, 24))
        copy(O("E", 0, n), by(O("ST"), O("fl%d" % t, *one)))
        tt(O("CC", 0, n), by(O("ST"), O("fl%d" % t, *two)), O("E", 0, n), LT)
        ex, ch = exchange(t), choose(t)
        for call in (ex[0], ch[0], ex[1], ch[1]):
            call()
        p = [lambda k=k: pick(t, k) for k in range(8)]
        if t == 1:
            walk(O("sb1"), 3, [ex[2:3], ex[3:4], ex[4:5] + ch[2:3], ch[3:4] + p[3:5], [p[0], p[1], p[2], p[5], p[6]], p[7:]])
        else:
            walk(O("sb%d" % t), 2, [ex[2:3], ex[3:4], ex[4:5] + ch[2:3], ch[3:4] + p[2:4], [p[0], p[1], p[4]], p[5:7], p[7:]])
        run("v", [O("SV")], [O("r8"), O("VV", 0, 320)],
            lambda: g.vector.tensor_tensor_scan(O("SV")[0], O("r8")[0], O("VV", 0, 320)[0], 0.0, MUL, ADD))
        ts(O("ml%d" % t), O("SV", 7, 320, 8), 160.0, None, ADD)
        k = send(t, O("ll%d" % t), O("ml%d" % t), "rl%d" % t)
        arrives("rl%d" % t, k, [O("ll%d" % t)])
        spread("own%d" % t, "al%d" % t, "ml%d" % t, "y")
        if t < 2:
            if t == 0:
                copy(O("y1"), P_by(2), "s")
            sp, df, vf = ahead(t + 1), differences(t + 1), [lambda k=k: score_places(t, k) for k in range(8)]
            for call in (df[1:2] + sp[0:1] + vf[0:2] + sp[1:2] + vf[2:4] + sp[2:3] + df[2:3] + sp[3:5] + df[3:4] + vf[4:5] + sp[5:6] + vf[5:7]
                         + sp[7:9] + vf[7:8] + sp[6:7] + df[0:1]):
                call()
            score_list(t + 1)
            sp[9]()
        else:
            scan(O("SF"), O("r16"), O("N"))
            ts(O("ls0"), O("SF", 15, 384, 16), -160.0, 1.0 / 320.0, ADD, MUL)
            ts(O("ls1"), O("ls0"), -1.0, O("h8"), MUL, ADD)
            ts(O("ls2"), O("ls1"), 7, None, AND)
            copy(O("gw"), O("ls2"))
            tt(O("o1"), by(O("wone"), O("gw")), O("lm"), MUL)
            tt(O("o2"), O("o1", 0, 192), O("o1", 192, 384), ADD)
            tt(O("o3"), O("o2", 0, 96), O("o2", 96, 192), ADD)
            tt(O("o4"), O("o3", 0, 48), O("o3", 48, 96), ADD)
            copy(O("ol40"), O("o4", 0, 40))
        tt(O("BG"), by(O("P", 0, 320), O("al%d" % t)), O("msk", 0, 320), SUB)
        scan(O("BS"), O("r16", 0, 320), O("BG"))
        ts(O("bl%d" % t), O("BS", 15, 320, 16), 160.0, None, ADD)
        spread("par%d" % t, "pl%d" % t, "ll%d" % t, "ys")
        if t == 2:
            spread("do1", "ow", "ol40", "y")
        for lo, hi in CH:
            off = O("pl%d" % t, lo // 16, hi // 16)
            for b in range(4):
                copy(O("zt%d" % t, 4 * lo + b, 4 * hi, 4), by(O("fp%d" % t, 320 * b, 320 * b + 320), off), "v" if b < 2 else "s")
            quant("zc%d" % t, "zs%d" % t, "zt%d" % t, lo, hi)
        if t == 0:
            quant("vq", "vqs", "vt", 0, 128)
            copy(O("xf"), O("xi"))
            ts(O("lm"), O("lm"), O("xf"), None, EQ)
        for lo, hi in CH:
            for b in range(4):
                p = mx("wq", 128 * b, "zc%d" % t, lo, hi, "zs%d" % t)
                o = O("rb%d" % b, lo, hi)
                run("s", [o], [p], lambda o=o, p=p: g.scalar.activation(o[0], p[0], COPY, scale=0.03125))
        for i, (lo, hi) in enumerate(CH):
            off = O("bl%d" % t, lo // 16, hi // 16)
            for b in range(4):
                tt(O("xt%d" % (t + 1), 4 * lo + b, 4 * hi, 4), by(O("rb%d" % b), off), O("fo%d" % t, 320 * b + lo, 320 * b + hi), ADD)
            quant("qc%d" % (t + 1), "qs%d" % (t + 1), "xt%d" % (t + 1), lo, hi)
            if t < 2 and i == 0:
                scores(t + 1, 0)
        if t < 2:
            send_state(t + 1)
            scores(t + 1, 1)
        else:
            copy(O("olf"), by(O("wone"), O("ow")))
    outs = []
    for lo, hi in CH:
        o = O("qc3", lo, hi)
        outs.append(("y", T.oc[:, 4 * lo:4 * hi], codes(o)[0], [], o[1]))
    for k in range(4):
        outs.append(("y", T.osc[4 * k:4 * k + 4, 0:320], T.qs3[32 * k:32 * k + 4, 0:320], [], O("qs3")[1]))
    outs.append(("y", T.ol[:], T.olf[0:128:16, 0:320], [], O("olf")[1]))
    for lo, hi in CH:
        p = mx("vq", 0, "qc3", lo, hi, "qs3")
        o = O("yb", lo, hi)
        copy(o, p, "s")
        outs.append(("s", T.y[:, lo:hi], o[0], [], o[1]))
    dmas("dout", outs)
    for s in SEMAPHORES:
        if total[s]:
            g.wait_ge(T.sem[s], total[s])
